import numpy as np
import ml_dtypes


def mxq(x, axis, fmt="e4m3"):
    dtype, down = {"e4m3": (ml_dtypes.float8_e4m3fn, 7), "e5m2": (ml_dtypes.float8_e5m2, 14)}[fmt]
    v = np.moveaxis(np.asarray(x, np.float32).astype(ml_dtypes.bfloat16).astype(np.float64), axis, -1)
    blocks = v.reshape(v.shape[:-1] + (-1, 32))
    amax = np.abs(blocks).max(-1, keepdims=True)
    byte = np.maximum(np.where(amax > 0, np.frexp(amax)[1] - 1 + 127, 0) - down, 1)
    scale = np.exp2(byte - 127.0)
    codes = (blocks / scale).astype(np.float32).astype(dtype).astype(np.float64)
    return np.moveaxis((codes * scale).reshape(v.shape), -1, axis)


WIDE = False


def mx_kscale(k):
    if not WIDE:
        return np.ones(k)
    levels = np.array([10, -10, 5, -5, 0])
    if k % 512:
        return np.exp2(np.random.permutation(np.resize(levels, k // 32))).repeat(32)
    a = np.empty((k // 512, 16))
    for p in range(k // 512):
        a[p, :8] = np.random.permutation(np.resize(levels, 8))
        for g in range(8):
            far = levels[np.abs(levels - a[p, g]) >= 10]
            a[p, g + 8] = far[np.random.randint(len(far))]
    return np.exp2(a.ravel()).repeat(32)


BF16 = ml_dtypes.bfloat16


def bf(x):
    return np.asarray(x, np.float32).astype(BF16)


def f64(x):
    return np.asarray(x).astype(np.float64)


E2M1 = np.array([0.0, 0.5, 1.0, 1.5, 2.0, 3.0, 4.0, 6.0, -0.0, -0.5, -1.0, -1.5, -2.0, -3.0, -4.0, -6.0])


def pack_weight(w, fmt):
    k, n = w.shape
    w = f64(bf(w)).reshape(k // 32, 32, n)
    amax = np.abs(w).max(1)
    if fmt == "e4m3":
        byte = np.frexp(amax)[1] - 1 + 127 - 7
    else:
        mant, ex = np.frexp(amax / 6.0)
        byte = np.where(mant > 0.5, ex, ex - 1) + 127
    byte = np.clip(np.where(amax > 0, byte, 1), 1, 254)
    scaled = (w * np.exp2(127.0 - byte)[:, None, :]).reshape(k, n).astype(np.float32)
    by_word = np.ascontiguousarray(scaled.reshape(k // 512, 128, 4, n).transpose(0, 1, 3, 2))
    if fmt == "e4m3":
        words = by_word.astype(ml_dtypes.float8_e4m3fn).view(np.uint8)
    else:
        c = by_word.astype(ml_dtypes.float4_e2m1fn).view(np.uint8) & 0xF
        words = c[..., 0::2] | (c[..., 1::2] << 4)
    return np.ascontiguousarray(words), np.ascontiguousarray(byte.astype(np.uint8).reshape(k // 512, 16, n))


def unpack_weight(words, scales, fmt):
    g, p, n, _ = words.shape
    if fmt == "e4m3":
        vals = np.ascontiguousarray(words).view(ml_dtypes.float8_e4m3fn).astype(np.float64)
    else:
        nib = np.empty((g, p, n, 4), np.uint8)
        nib[..., 0::2] = words & 0xF
        nib[..., 1::2] = words >> 4
        vals = E2M1[nib]
    vals = vals * np.repeat(np.exp2(scales.astype(np.float64) - 127.0), 8, axis=1)[..., None]
    return vals.transpose(0, 1, 3, 2).reshape(g * 512, n)
def pack4(w):
    words, scales = pack_weight(w, "e2m1")
    return words.reshape(words.shape[0], 128, -1), scales


def unpack4(words, scales):
    return unpack_weight(words.reshape(words.shape[0], 128, -1, 2), scales, "e2m1")


D, G, N = 640, 2560, 1024


def setup_inputs():
    s = mx_kscale(G)
    seeds = np.random.standard_normal((D, G)) * s
    far = np.random.standard_normal((G, N)) / np.sqrt(G) / s[:, None]
    walk = np.random.standard_normal((G, N)) / np.sqrt(G) / s[:, None]
    modules = np.random.standard_normal((G, N)) / np.sqrt(G) / s[:, None]
    far_words, far_scales = pack4(far)
    walk_words, walk_scales = pack_weight(walk, "e4m3")
    return {"seeds": bf(seeds),
            "far_words": far_words,
            "far_scales": far_scales,
            "walk_words": walk_words,
            "walk_scales": walk_scales,
            "modules": bf(modules)}


def reference(seeds, far_words, far_scales, walk_words, walk_scales, modules):
    x = mxq(f64(seeds), 1, "e4m3")
    far = unpack4(far_words, far_scales)
    walk = unpack_weight(walk_words, walk_scales, "e4m3")
    near = mxq(f64(modules), 0, "e4m3")
    diffused = x @ far
    odds = np.exp(x @ walk)
    direct = x @ near
    return diffused + (direct - diffused) / (1.0 + odds)

@@ -1,0 +1,329 @@
+from contextlib import ExitStack
+
+import concourse.mybir as mybir
+from concourse.masks import make_identity
+
+D, K, N = 640, 2560, 1024
+FLOPS = 3 * 2 * D * K * N
+
+F32 = mybir.dt.float32
+BF16 = mybir.dt.bfloat16
+U32 = mybir.dt.uint32
+I32 = mybir.dt.int32
+U8 = mybir.dt.uint8
+E4M3 = mybir.dt.float8_e4m3fn_x4
+E2M1 = mybir.dt.float4_e2m1fn_x4
+ALU = mybir.AluOpType
+SIGMOID = mybir.ActivationFunctionType.Sigmoid
+
+P = 128
+G = K // 512
+MT = D // P
+NH = 512
+H = N // NH
+
+
+def tile_drug_restart_scores_s10_kernel(
+    tc, seeds, far_words, far_scales, walk_words, walk_scales, modules, out
+):
+    nc = tc.nc
+    with ExitStack() as ctx:
+        keep = ctx.enter_context(tc.tile_pool(name="keep", bufs=1))
+        stage = ctx.enter_context(tc.tile_pool(name="stage", bufs=2))
+        psum = ctx.enter_context(tc.psum_pool(name="psum", bufs=8))
+        ctx.enter_context(tc.manual_schedule())
+
+        ident = keep.tile([P, P], F32, name="ident", align_bytes=256)
+        warm = keep.tile([P, 2], F32, name="warm", align_bytes=256)
+        x_raw = [keep.tile([P, K], BF16, name="x_raw%d" % m, align_bytes=256) for m in range(MT)]
+        x_codes = [keep.tile([P, G, P], U32, name="x_codes%d" % m, align_bytes=256) for m in range(MT)]
+        x_scales = [keep.tile([P, G, P], U8, name="x_scales%d" % m, align_bytes=256) for m in range(MT)]
+        f_words = keep.tile([P, G, 2 * N], U8, name="f_words", align_bytes=256)
+        f_scales = keep.tile([P, G, N], U8, name="f_scales", align_bytes=256)
+        w_words = keep.tile([P, G, N], U32, name="w_words", align_bytes=256)
+        w_scales = keep.tile([P, G, N], U8, name="w_scales", align_bytes=256)
+        d_raw = [[keep.tile([P, 4, NH], BF16, name="d_raw%d%d" % (g, h), align_bytes=256) for h in range(H)] for g in range(G)]
+        d_codes = keep.tile([P, G, N], U32, name="d_codes", align_bytes=256)
+        d_scales = keep.tile([P, G, N], U8, name="d_scales", align_bytes=256)
+        pairs = [(m, h) for h in range(H) for m in range(MT)]
+        f_sb = {mh: keep.tile([P, NH], F32, name="f_sb%d%d" % mh, align_bytes=256) for mh in pairs}
+        r_sb = {mh: keep.tile([P, NH], F32, name="r_sb%d%d" % mh, align_bytes=256) for mh in pairs}
+
+        def load_x(m, k0, k1):
+            nc.sync.dma_start(out=x_raw[m][:, k0:k1], in_=seeds[m * P : (m + 1) * P, k0:k1])
+
+        def load_far(g0, g1, h):
+            w = NH // 2
+            nc.sync.dma_start(
+                out=f_words[:].bitcast(I32)[:, g0:g1, h * w : (h + 1) * w],
+                in_=far_words.bitcast(I32)[g0:g1, :, h * w : (h + 1) * w].rearrange("g p w -> p g w"),
+            )
+
+        def load_walk(g0, g1, h):
+            words = walk_words.rearrange("g p n t -> g p (n t)").bitcast(I32)
+            nc.sync.dma_start(
+                out=w_words[:].bitcast(I32)[:, g0:g1, h * NH : (h + 1) * NH],
+                in_=words[g0:g1, :, h * NH : (h + 1) * NH].rearrange("g p w -> p g w"),
+            )
+
+        def load_scales(tile, dram):
+            for r in range(4):
+                nc.sync.dma_start(
+                    out=tile[:].bitcast(I32)[r:P:32, :, :],
+                    in_=dram.bitcast(I32)[:, r:16:4, :].rearrange("g q w -> q g w"),
+                )
+
+        def load_modules(g, h):
+            rows = modules[512 * g : 512 * (g + 1), h * NH : (h + 1) * NH]
+            nc.sync.dma_start(out=d_raw[g][h][:], in_=rows.rearrange("(p j) w -> p j w", j=4))
+
+        nc.gpsimd.memset(f_scales[:].bitcast(I32)[:, :, 0:128], 0)
+        nc.vector.memset(f_scales[:].bitcast(I32)[:, :, 128:256], 0)
+        nc.gpsimd.memset(d_codes[:, G - 1, 0:NH], 0)
+        nc.gpsimd.memset(d_scales[:, G - 1, 0:NH].bitcast(I32), 0)
+
+        def busy(count):
+            bank = psum.tile([P, NH], F32, name="bank")
+            for i in range(count):
+                nc.tensor.matmul_mx(
+                    out=bank[:],
+                    lhsT=d_codes[:, G - 1, 0:P].bitcast(E4M3),
+                    lhsT_scale=d_scales[:, G - 1, 0:P],
+                    rhs=d_codes[:, G - 1, 0:NH].bitcast(E4M3),
+                    rhs_scale=d_scales[:, G - 1, 0:NH],
+                    start=True,
+                    stop=True,
+                )
+
+
+        nc.vector.memset(warm[:], 0.0)
+        nc.vector.memset(w_scales[:].bitcast(I32), 0)
+        make_identity(nc, ident[:])
+        nc.scalar.activation(out=warm[:, 1:2], in_=warm[:, 0:1], func=SIGMOID)
+
+        load_x(0, 0, 1024)
+        load_scales(f_scales, far_scales)
+        load_far(0, 2, 0)
+        load_x(0, 1024, K)
+        load_far(2, 5, 0)
+        load_x(1, 0, K)
+        load_far(0, 5, 1)
+        load_x(2, 0, K)
+        load_modules(0, 0)
+        load_x(3, 0, K)
+        load_x(4, 0, K)
+        load_scales(w_scales, walk_scales)
+        load_modules(1, 0)
+        load_walk(0, 5, 0)
+        load_modules(2, 0)
+        load_modules(3, 0)
+        load_modules(4, 0)
+        load_modules(0, 1)
+        load_modules(1, 1)
+        load_walk(0, 5, 1)
+        load_modules(2, 1)
+        load_modules(3, 1)
+        load_modules(4, 1)
+
+        spans = [(0, 2), (2, 4), (4, 5)]
+        banks = {}
+        grouped = {}
+        ordered = {}
+
+        def reorder_x(m, engine_copy):
+            t = stage.tile([P, G, 2, P], F32, name="x_ordered", align_bytes=256)
+            engine_copy(out=t[:], in_=x_raw[m][:].bitcast(F32).rearrange("r (g p u) -> r g u p", u=2, p=P))
+            ordered[m] = t
+
+        def transpose_x(m, s):
+            g0, g1 = spans[s]
+            bank = psum.tile([P, 2, 2, P], F32, name="bank")
+            for g in range(g0, g1):
+                for u in range(2):
+                    if m in ordered:
+                        src = ordered[m][:, g, u, :]
+                    else:
+                        src = x_raw[m][:].bitcast(F32)[:, 256 * g + u : 256 * (g + 1) : 2]
+                    nc.tensor.transpose(bank[:, g - g0, u, :], src, ident[:])
+            banks[m, s] = bank
+
+        def copy_x(m, s, engine_copy):
+            g0, g1 = spans[s]
+            t = stage.tile([P, 2, P, 4], BF16, name="x_grouped%d" % s, align_bytes=256)
+            n = g1 - g0
+            engine_copy(
+                out=t[:].bitcast(F32)[:, 0:n, :, :], in_=banks[m, s][:, 0:n, :, :].rearrange("p g u r -> p g r u")
+            )
+            grouped[m, s] = t
+
+        def quantize_x(m, s):
+            g0, g1 = spans[s]
+            n = g1 - g0
+            nc.vector.quantize_mx(
+                out=x_codes[m][:, g0:g1, :].rearrange("p g r -> p (g r)").bitcast(E4M3),
+                scales=x_scales[m][:, g0:g1, :].rearrange("p g r -> p (g r)"),
+                in_=grouped[m, s][:, 0:n, :, :].rearrange("p g r j -> p (g r j)"),
+            )
+
+        vcopy = nc.vector.tensor_copy
+        scopy = nc.scalar.copy
+
+        d_grouped = {}
+
+        def copy_d(g, h, engine_copy, c0=0, c1=NH):
+            if c0 == 0:
+                d_grouped[g, h] = stage.tile([P, NH, 4], BF16, name="d_grouped", align_bytes=256, bufs=4)
+            engine_copy(
+                out=d_grouped[g, h][:, c0:c1, :].rearrange("p (c i) j -> p c j i", i=4),
+                in_=d_raw[g][h][:, :, c0:c1].rearrange("p j (c i) -> p c j i", i=4),
+            )
+
+        def quantize_d(g, h):
+            cols = slice(h * NH, (h + 1) * NH)
+            nc.vector.quantize_mx(
+                out=d_codes[:, g, cols].bitcast(E4M3),
+                scales=d_scales[:, g, cols],
+                in_=d_grouped[g, h][:].rearrange("p w j -> p (w j)"),
+            )
+
+        acc = {}
+
+        def product(kind, m, h, c0=0, c1=NH):
+            bank = psum.tile([P, NH], F32, name="bank")
+            n0, n1 = h * NH + c0, h * NH + c1
+            for g in range(G):
+                if kind == "far":
+                    rhs, scale = f_words[:, g, 2 * n0 : 2 * n1].bitcast(E2M1), f_scales[:, g, n0:n1]
+                elif kind == "walk":
+                    rhs, scale = w_words[:, g, n0:n1].bitcast(E4M3), w_scales[:, g, n0:n1]
+                else:
+                    rhs, scale = d_codes[:, g, n0:n1].bitcast(E4M3), d_scales[:, g, n0:n1]
+                nc.tensor.matmul_mx(
+                    out=bank[:, c0:c1],
+                    lhsT=x_codes[m][:, g, :].bitcast(E4M3),
+                    lhsT_scale=x_scales[m][:, g, :],
+                    rhs=rhs,
+                    rhs_scale=scale,
+                    start=(g == 0),
+                    stop=(g == G - 1),
+                )
+            acc[kind, m, h, c0] = bank
+
+        def keep_far(m, h):
+            nc.scalar.copy(out=f_sb[m, h][:], in_=acc["far", m, h, 0][:])
+
+        def restart(m, h):
+            nc.scalar.activation(out=r_sb[m, h][:], in_=acc["walk", m, h, 0][:], func=SIGMOID, scale=-1.0)
+
+        def weigh_far(m, h):
+            nc.vector.scalar_tensor_tensor(
+                out=f_sb[m, h][:], in0=r_sb[m, h][:], scalar=1.0, in1=f_sb[m, h][:], op0=ALU.subtract, op1=ALU.mult
+            )
+
+        def weigh_direct(m, h, c0=0, c1=NH):
+            r = r_sb[m, h][:, c0:c1]
+            nc.vector.tensor_tensor(out=r, in0=acc["direct", m, h, c0][:, c0:c1], in1=r, op=ALU.mult)
+
+        def add_up(m, h, c0=0, c1=NH):
+            r = r_sb[m, h][:, c0:c1]
+            nc.vector.tensor_tensor(out=r, in0=r, in1=f_sb[m, h][:, c0:c1], op=ALU.subtract)
+            nc.sync.dma_start(out=out[m * P : (m + 1) * P, h * NH + c0 : h * NH + c1], in_=r)
+
+        transpose_x(0, 0)
+        busy(2)
+        transpose_x(0, 1)
+        transpose_x(0, 2)
+        copy_x(0, 0, vcopy)
+        copy_x(0, 1, scopy)
+        quantize_x(0, 0)
+        copy_x(0, 2, vcopy)
+        quantize_x(0, 1)
+        quantize_x(0, 2)
+
+        def bring_x(m):
+            for s in range(3):
+                transpose_x(m, s)
+
+        def take_x(m):
+            copy_x(m, 0, vcopy)
+            copy_x(m, 1, scopy)
+            copy_x(m, 2, vcopy)
+            for s in range(3):
+                quantize_x(m, s)
+
+        product("far", 0, 0)
+        reorder_x(1, vcopy)
+        bring_x(1)
+        take_x(1)
+        product("far", 0, 1)
+        keep_far(0, 0)
+        product("far", 1, 0)
+        reorder_x(2, scopy)
+        keep_far(0, 1)
+        bring_x(2)
+        take_x(2)
+        product("far", 1, 1)
+        reorder_x(3, scopy)
+        reorder_x(4, vcopy)
+        copy_d(0, 0, vcopy)
+        keep_far(1, 0)
+        product("far", 2, 0)
+        keep_far(1, 1)
+        bring_x(3)
+        take_x(3)
+        bring_x(4)
+        take_x(4)
+        product("far", 2, 1)
+        keep_far(2, 0)
+        quantize_d(0, 0)
+        product("far", 3, 0)
+        keep_far(2, 1)
+        copy_d(1, 0, scopy)
+        copy_d(2, 0, vcopy)
+        product("far", 3, 1)
+        keep_far(3, 0)
+        quantize_d(1, 0)
+        quantize_d(2, 0)
+        product("far", 4, 0)
+        keep_far(3, 1)
+        copy_d(3, 0, scopy)
+        product("far", 4, 1)
+        keep_far(4, 0)
+        copy_d(4, 0, vcopy)
+
+        steps = [(kind, m, h) for h in range(H) for kind in ("walk", "direct") for m in range(MT)]
+        last = len(steps) - 1
+        scalar_parts = {3: (1, 0), 4: (1, 1), 6: (2, 0), 7: (2, 1), 8: (3, 0), 9: (3, 1), 10: (4, 0), 11: (4, 1)}
+        vector_chunks = {1: (0, 1)}
+        quantize_at = {0: [(3, 0)], 1: [(4, 0)], 2: [(0, 1)], 6: [(1, 1)], 9: [(2, 1)], 11: [(3, 1)], 13: [(4, 1)]}
+        for s, (kind, m, h) in enumerate(steps):
+            if s < last:
+                product(kind, m, h)
+            else:
+                product(kind, m, h, 0, 256)
+                product(kind, m, h, 256, 512)
+            if s == 0:
+                keep_far(4, 1)
+            elif steps[s - 1][0] == "walk":
+                restart(*steps[s - 1][1:])
+            if s in vector_chunks:
+                copy_d(*vector_chunks[s], vcopy)
+            if s in scalar_parts:
+                g, part = scalar_parts[s]
+                copy_d(g, 1, scopy, 256 * part, 256 * (part + 1))
+            for chunk in quantize_at.get(s, []):
+                quantize_d(*chunk)
+            if s >= 2:
+                before, mb, hb = steps[s - 2]
+                if before == "walk":
+                    weigh_far(mb, hb)
+                else:
+                    add_up(mb, hb)
+            if s >= 1 and steps[s - 1][0] == "direct":
+                weigh_direct(*steps[s - 1][1:])
+        m, h = steps[last][1:]
+        weigh_direct(m, h, 0, 256)
+        add_up(m - 1, h)
+        weigh_direct(m, h, 256, 512)
+        add_up(m, h, 0, 256)
+        add_up(m, h, 256, 512)

@@ -34,7 +34,6 @@ def tile_drug_restart_scores_s10_kernel(
         ctx.enter_context(tc.manual_schedule())
 
         ident = keep.tile([P, P], F32, name="ident", align_bytes=256)
-        warm = keep.tile([P, 2], F32, name="warm", align_bytes=256)
         x_raw = [keep.tile([P, K], BF16, name="x_raw%d" % m, align_bytes=256) for m in range(MT)]
         x_codes = [keep.tile([P, G, P], U32, name="x_codes%d" % m, align_bytes=256) for m in range(MT)]
         x_scales = [keep.tile([P, G, P], U8, name="x_scales%d" % m, align_bytes=256) for m in range(MT)]
@@ -79,27 +78,9 @@ def tile_drug_restart_scores_s10_kernel(
 
         nc.gpsimd.memset(f_scales[:].bitcast(I32)[:, :, 0:128], 0)
         nc.vector.memset(f_scales[:].bitcast(I32)[:, :, 128:256], 0)
-        nc.gpsimd.memset(d_codes[:, G - 1, 0:NH], 0)
-        nc.gpsimd.memset(d_scales[:, G - 1, 0:NH].bitcast(I32), 0)
 
-        def busy(count):
-            bank = psum.tile([P, NH], F32, name="bank")
-            for i in range(count):
-                nc.tensor.matmul_mx(
-                    out=bank[:],
-                    lhsT=d_codes[:, G - 1, 0:P].bitcast(E4M3),
-                    lhsT_scale=d_scales[:, G - 1, 0:P],
-                    rhs=d_codes[:, G - 1, 0:NH].bitcast(E4M3),
-                    rhs_scale=d_scales[:, G - 1, 0:NH],
-                    start=True,
-                    stop=True,
-                )
-
-
-        nc.vector.memset(warm[:], 0.0)
         nc.vector.memset(w_scales[:].bitcast(I32), 0)
         make_identity(nc, ident[:])
-        nc.scalar.activation(out=warm[:, 1:2], in_=warm[:, 0:1], func=SIGMOID)
 
         load_x(0, 0, 1024)
         load_scales(f_scales, far_scales)
@@ -230,7 +211,6 @@ def tile_drug_restart_scores_s10_kernel(
             nc.sync.dma_start(out=out[m * P : (m + 1) * P, h * NH + c0 : h * NH + c1], in_=r)
 
         transpose_x(0, 0)
-        busy(2)
         transpose_x(0, 1)
         transpose_x(0, 2)
         copy_x(0, 0, vcopy)

@@ -14,13 +14,15 @@ U8 = mybir.dt.uint8
 E4M3 = mybir.dt.float8_e4m3fn_x4
 E2M1 = mybir.dt.float4_e2m1fn_x4
 ALU = mybir.AluOpType
-SIGMOID = mybir.ActivationFunctionType.Sigmoid
+TANH = mybir.ActivationFunctionType.Tanh
+COPY = mybir.ActivationFunctionType.Copy
 
 P = 128
 G = K // 512
 MT = D // P
 NH = 512
 H = N // NH
+RUNS = [(0, 1), (1, 3), (3, 5)]
 
 
 def tile_drug_restart_scores_s10_kernel(
@@ -30,17 +32,18 @@ def tile_drug_restart_scores_s10_kernel(
     with ExitStack() as ctx:
         keep = ctx.enter_context(tc.tile_pool(name="keep", bufs=1))
         stage = ctx.enter_context(tc.tile_pool(name="stage", bufs=2))
-        psum = ctx.enter_context(tc.psum_pool(name="psum", bufs=8))
+        psum = ctx.enter_context(tc.psum_pool(name="psum", bufs=1))
         ctx.enter_context(tc.manual_schedule())
+        vcopy = nc.vector.tensor_copy
+        scopy = nc.scalar.copy
 
         ident = keep.tile([P, P], F32, name="ident", align_bytes=256)
-        x_raw = [keep.tile([P, K], BF16, name="x_raw%d" % m, align_bytes=256) for m in range(MT)]
         x_codes = [keep.tile([P, G, P], U32, name="x_codes%d" % m, align_bytes=256) for m in range(MT)]
         x_scales = [keep.tile([P, G, P], U8, name="x_scales%d" % m, align_bytes=256) for m in range(MT)]
-        f_words = keep.tile([P, G, 2 * N], U8, name="f_words", align_bytes=256)
-        f_scales = keep.tile([P, G, N], U8, name="f_scales", align_bytes=256)
-        w_words = keep.tile([P, G, N], U32, name="w_words", align_bytes=256)
-        w_scales = keep.tile([P, G, N], U8, name="w_scales", align_bytes=256)
+        f_words = [keep.tile([P, 2 * N], U8, name="f_words%d" % g, align_bytes=256) for g in range(G)]
+        f_scales = {g0: keep.tile([P, g1 - g0, N], U8, name="f_scales%d" % g0, align_bytes=256) for g0, g1 in RUNS}
+        w_words = [keep.tile([P, G, NH], U32, name="w_words%d" % h, align_bytes=256) for h in range(H)]
+        w_scales = [keep.tile([P, N], U8, name="w_scales%d" % i, align_bytes=256) for i in range(2)]
         d_raw = [[keep.tile([P, 4, NH], BF16, name="d_raw%d%d" % (g, h), align_bytes=256) for h in range(H)] for g in range(G)]
         d_codes = keep.tile([P, G, N], U32, name="d_codes", align_bytes=256)
         d_scales = keep.tile([P, G, N], U8, name="d_scales", align_bytes=256)
@@ -48,106 +51,134 @@ def tile_drug_restart_scores_s10_kernel(
         f_sb = {mh: keep.tile([P, NH], F32, name="f_sb%d%d" % mh, align_bytes=256) for mh in pairs}
         r_sb = {mh: keep.tile([P, NH], F32, name="r_sb%d%d" % mh, align_bytes=256) for mh in pairs}
 
-        def load_x(m, k0, k1):
-            nc.sync.dma_start(out=x_raw[m][:, k0:k1], in_=seeds[m * P : (m + 1) * P, k0:k1])
+        x_raw = {}
 
-        def load_far(g0, g1, h):
-            w = NH // 2
-            nc.sync.dma_start(
-                out=f_words[:].bitcast(I32)[:, g0:g1, h * w : (h + 1) * w],
-                in_=far_words.bitcast(I32)[g0:g1, :, h * w : (h + 1) * w].rearrange("g p w -> p g w"),
-            )
+        def load_x(m0, m1, g0, g1):
+            t = keep.tile([P, m1 - m0, 512 * (g1 - g0)], BF16, name="x_raw%d%d" % (m0, g0), align_bytes=256)
+            rows = seeds[m0 * P : m1 * P, 512 * g0 : 512 * g1]
+            nc.sync.dma_start(out=t[:], in_=rows.rearrange("(m p) k -> p m k", p=P))
+            words = t[:].rearrange("p m k -> p (m k)").bitcast(F32)
+            for m in range(m0, m1):
+                for g in range(g0, g1):
+                    x_raw[m, g] = (words, 256 * ((m - m0) * (g1 - g0) + g - g0))
+
+        def load_far(g):
+            nc.sync.dma_start(out=f_words[g][:].bitcast(I32), in_=far_words.bitcast(I32)[g])
 
         def load_walk(g0, g1, h):
             words = walk_words.rearrange("g p n t -> g p (n t)").bitcast(I32)
             nc.sync.dma_start(
-                out=w_words[:].bitcast(I32)[:, g0:g1, h * NH : (h + 1) * NH],
+                out=w_words[h][:].bitcast(I32)[:, g0:g1, :],
                 in_=words[g0:g1, :, h * NH : (h + 1) * NH].rearrange("g p w -> p g w"),
             )
 
-        def load_scales(tile, dram):
+        def load_far_scales(g0, g1):
             for r in range(4):
                 nc.sync.dma_start(
-                    out=tile[:].bitcast(I32)[r:P:32, :, :],
-                    in_=dram.bitcast(I32)[:, r:16:4, :].rearrange("g q w -> q g w"),
+                    out=f_scales[g0][:].bitcast(I32)[r:P:32, :, :],
+                    in_=far_scales.bitcast(I32)[g0:g1, r:16:4, :].rearrange("g q w -> q g w"),
+                )
+
+        def load_walk_scales_packed():
+            for q in range(4):
+                nc.sync.dma_start(
+                    out=w_scales[0][:].bitcast(I32)[32 * q : 32 * q + 16, :],
+                    in_=walk_scales.bitcast(I32)[0:4, 4 * q : 4 * q + 4, :],
+                )
+
+        def load_walk_scales_last():
+            for r in range(4):
+                nc.sync.dma_start(
+                    out=w_scales[1][:].bitcast(I32)[r:P:32, :], in_=walk_scales.bitcast(I32)[4, r:16:4, :]
                 )
 
         def load_modules(g, h):
             rows = modules[512 * g : 512 * (g + 1), h * NH : (h + 1) * NH]
             nc.sync.dma_start(out=d_raw[g][h][:], in_=rows.rearrange("(p j) w -> p j w", j=4))
 
-        nc.gpsimd.memset(f_scales[:].bitcast(I32)[:, :, 0:128], 0)
-        nc.vector.memset(f_scales[:].bitcast(I32)[:, :, 128:256], 0)
-
-        nc.vector.memset(w_scales[:].bitcast(I32), 0)
+        nc.gpsimd.memset(f_scales[0][:].bitcast(I32), 0)
         make_identity(nc, ident[:])
+        nc.vector.memset(f_scales[1][:].bitcast(I32), 0)
+        nc.vector.memset(f_scales[3][:].bitcast(I32), 0)
+        nc.vector.memset(w_scales[0][:].bitcast(I32), 0)
+        nc.vector.memset(w_scales[1][:].bitcast(I32), 0)
 
-        load_x(0, 0, 1024)
-        load_scales(f_scales, far_scales)
-        load_far(0, 2, 0)
-        load_x(0, 1024, K)
-        load_far(2, 5, 0)
-        load_x(1, 0, K)
-        load_far(0, 5, 1)
-        load_x(2, 0, K)
+        load_x(0, 2, 0, 1)
+        load_far_scales(0, 1)
+        load_far(0)
+        load_x(2, 3, 0, 1)
+        load_x(0, 1, 1, 3)
+        load_far_scales(1, 3)
+        load_far(1)
+        load_x(1, 2, 1, 3)
+        load_far(2)
+        load_x(2, 3, 1, 3)
+        load_x(0, 1, 3, 5)
+        load_far_scales(3, 5)
+        load_x(1, 2, 3, 5)
+        load_far(3)
+        load_x(2, 3, 3, 5)
+        load_far(4)
+        load_x(3, 4, 0, 5)
         load_modules(0, 0)
-        load_x(3, 0, K)
-        load_x(4, 0, K)
-        load_scales(w_scales, walk_scales)
+        load_x(4, 5, 0, 5)
+        load_walk_scales_packed()
+        load_walk_scales_last()
         load_modules(1, 0)
-        load_walk(0, 5, 0)
         load_modules(2, 0)
+        load_walk(0, 5, 0)
         load_modules(3, 0)
         load_modules(4, 0)
         load_modules(0, 1)
         load_modules(1, 1)
-        load_walk(0, 5, 1)
         load_modules(2, 1)
+        load_walk(0, 5, 1)
         load_modules(3, 1)
         load_modules(4, 1)
 
-        spans = [(0, 2), (2, 4), (4, 5)]
-        banks = {}
-        grouped = {}
         ordered = {}
+        turned = {}
+        grouped = {}
 
-        def reorder_x(m, engine_copy):
-            t = stage.tile([P, G, 2, P], F32, name="x_ordered", align_bytes=256)
-            engine_copy(out=t[:], in_=x_raw[m][:].bitcast(F32).rearrange("r (g p u) -> r g u p", u=2, p=P))
-            ordered[m] = t
+        def reorder_x(chunks, engine_copy):
+            n = len(chunks)
+            t = stage.tile([P, n, 2, P], F32, name="x_ordered%d" % n, align_bytes=256)
+            words, w0 = x_raw[chunks[0]]
+            engine_copy(out=t[:], in_=words[:, w0 : w0 + 256 * n].rearrange("r (c p u) -> r c u p", u=2, p=P))
+            for i, c in enumerate(chunks):
+                ordered[c] = (t, i)
 
-        def transpose_x(m, s):
-            g0, g1 = spans[s]
-            bank = psum.tile([P, 2, 2, P], F32, name="bank")
-            for g in range(g0, g1):
+        def transpose_x(chunks, b):
+            bank = psum.tile([P, 2, 2, P], F32, name="bank%d" % b)
+            for j, c in enumerate(chunks):
                 for u in range(2):
-                    if m in ordered:
-                        src = ordered[m][:, g, u, :]
+                    if c in ordered:
+                        t, i = ordered[c]
+                        src = t[:, i, u, :]
                     else:
-                        src = x_raw[m][:].bitcast(F32)[:, 256 * g + u : 256 * (g + 1) : 2]
-                    nc.tensor.transpose(bank[:, g - g0, u, :], src, ident[:])
-            banks[m, s] = bank
+                        words, w0 = x_raw[c]
+                        src = words[:, w0 + u : w0 + 256 : 2]
+                    nc.tensor.transpose(bank[:, j, u, :], src, ident[:])
+            turned[chunks[0]] = bank
 
-        def copy_x(m, s, engine_copy):
-            g0, g1 = spans[s]
-            t = stage.tile([P, 2, P, 4], BF16, name="x_grouped%d" % s, align_bytes=256)
-            n = g1 - g0
-            engine_copy(
-                out=t[:].bitcast(F32)[:, 0:n, :, :], in_=banks[m, s][:, 0:n, :, :].rearrange("p g u r -> p g r u")
-            )
-            grouped[m, s] = t
+        def copy_x(chunks, engine_copy):
+            n = len(chunks)
+            t = stage.tile([P, 2, P, 4], BF16, name="x_grouped", align_bytes=256, bufs=4)
+            engine_copy(out=t[:].bitcast(F32)[:, 0:n], in_=turned[chunks[0]][:, 0:n, :, :].rearrange("p c u r -> p c r u"))
+            grouped[chunks[0]] = t
 
-        def quantize_x(m, s):
-            g0, g1 = spans[s]
-            n = g1 - g0
+        def x_operand(m, g):
+            return x_codes[m][:, g, :], x_scales[m][:, g, :]
+
+        def quantize_x(chunks):
+            n = len(chunks)
+            m, g = chunks[0]
+            codes, scales = x_codes[m][:, g : g + n, :], x_scales[m][:, g : g + n, :]
             nc.vector.quantize_mx(
-                out=x_codes[m][:, g0:g1, :].rearrange("p g r -> p (g r)").bitcast(E4M3),
-                scales=x_scales[m][:, g0:g1, :].rearrange("p g r -> p (g r)"),
-                in_=grouped[m, s][:, 0:n, :, :].rearrange("p g r j -> p (g r j)"),
+                out=codes.rearrange("p c r -> p (c r)").bitcast(E4M3),
+                scales=scales.rearrange("p c r -> p (c r)"),
+                in_=grouped[chunks[0]][:, 0:n].rearrange("p c r j -> p (c r j)"),
             )
-
-        vcopy = nc.vector.tensor_copy
-        scopy = nc.scalar.copy
 
         d_grouped = {}
 
@@ -169,141 +200,169 @@ def tile_drug_restart_scores_s10_kernel(
 
         acc = {}
 
-        def product(kind, m, h, c0=0, c1=NH):
-            bank = psum.tile([P, NH], F32, name="bank")
+        def one_pass(kind, m, h, g, c0=0, c1=NH):
             n0, n1 = h * NH + c0, h * NH + c1
+            if kind == "far":
+                g0 = max(a for a, b in RUNS if a <= g)
+                rhs, scale = f_words[g][:, 2 * n0 : 2 * n1].bitcast(E2M1), f_scales[g0][:, g - g0, n0:n1]
+            elif kind == "walk":
+                rhs = w_words[h][:, g, c0:c1].bitcast(E4M3)
+                scale = w_scales[g // 4][4 * (g % 4) :, n0:n1]
+            else:
+                rhs, scale = d_codes[:, g, n0:n1].bitcast(E4M3), d_scales[:, g, n0:n1]
+            codes, scales = x_operand(m, g)
+            nc.tensor.matmul_mx(
+                out=acc[kind, m, h, c0][:, c0:c1],
+                lhsT=codes.bitcast(E4M3),
+                lhsT_scale=scales,
+                rhs=rhs,
+                rhs_scale=scale,
+                start=(g == 0),
+                stop=(g == G - 1),
+            )
+
+        def product(kind, m, h, bank, c0=0, c1=NH):
+            acc[kind, m, h, c0] = psum.tile([P, NH], F32, name="bank%d" % bank)
             for g in range(G):
-                if kind == "far":
-                    rhs, scale = f_words[:, g, 2 * n0 : 2 * n1].bitcast(E2M1), f_scales[:, g, n0:n1]
-                elif kind == "walk":
-                    rhs, scale = w_words[:, g, n0:n1].bitcast(E4M3), w_scales[:, g, n0:n1]
-                else:
-                    rhs, scale = d_codes[:, g, n0:n1].bitcast(E4M3), d_scales[:, g, n0:n1]
-                nc.tensor.matmul_mx(
-                    out=bank[:, c0:c1],
-                    lhsT=x_codes[m][:, g, :].bitcast(E4M3),
-                    lhsT_scale=x_scales[m][:, g, :],
-                    rhs=rhs,
-                    rhs_scale=scale,
-                    start=(g == 0),
-                    stop=(g == G - 1),
-                )
-            acc[kind, m, h, c0] = bank
+                one_pass(kind, m, h, g, c0, c1)
 
         def keep_far(m, h):
-            nc.scalar.copy(out=f_sb[m, h][:], in_=acc["far", m, h, 0][:])
+            nc.scalar.activation(out=f_sb[m, h][:], in_=acc["far", m, h, 0][:], func=COPY, scale=0.5)
 
         def restart(m, h):
-            nc.scalar.activation(out=r_sb[m, h][:], in_=acc["walk", m, h, 0][:], func=SIGMOID, scale=-1.0)
+            nc.scalar.activation(out=r_sb[m, h][:], in_=acc["walk", m, h, 0][:], func=TANH, scale=0.5)
 
         def weigh_far(m, h):
             nc.vector.scalar_tensor_tensor(
-                out=f_sb[m, h][:], in0=r_sb[m, h][:], scalar=1.0, in1=f_sb[m, h][:], op0=ALU.subtract, op1=ALU.mult
+                out=f_sb[m, h][:], in0=r_sb[m, h][:], scalar=1.0, in1=f_sb[m, h][:], op0=ALU.add, op1=ALU.mult
             )
 
-        def weigh_direct(m, h, c0=0, c1=NH):
+        def weigh_direct(m, h, c0, c1, group=0):
             r = r_sb[m, h][:, c0:c1]
-            nc.vector.tensor_tensor(out=r, in0=acc["direct", m, h, c0][:, c0:c1], in1=r, op=ALU.mult)
+            nc.vector.scalar_tensor_tensor(
+                out=r, in0=r, scalar=1.0, in1=acc["direct", m, h, group][:, c0:c1], op0=ALU.subtract, op1=ALU.mult
+            )
 
-        def add_up(m, h, c0=0, c1=NH):
+        def add_up(m, h, c0, c1):
             r = r_sb[m, h][:, c0:c1]
-            nc.vector.tensor_tensor(out=r, in0=r, in1=f_sb[m, h][:, c0:c1], op=ALU.subtract)
-            nc.sync.dma_start(out=out[m * P : (m + 1) * P, h * NH + c0 : h * NH + c1], in_=r)
+            nc.vector.scalar_tensor_tensor(
+                out=r, in0=r, scalar=-0.5, in1=f_sb[m, h][:, c0:c1], op0=ALU.mult, op1=ALU.add
+            )
 
-        transpose_x(0, 0)
-        transpose_x(0, 1)
-        transpose_x(0, 2)
-        copy_x(0, 0, vcopy)
-        copy_x(0, 1, scopy)
-        quantize_x(0, 0)
-        copy_x(0, 2, vcopy)
-        quantize_x(0, 1)
-        quantize_x(0, 2)
+        def store(m, h, c0, c1):
+            nc.sync.dma_start(out=out[m * P : (m + 1) * P, h * NH + c0 : h * NH + c1], in_=r_sb[m, h][:, c0:c1])
 
-        def bring_x(m):
-            for s in range(3):
-                transpose_x(m, s)
+        def finish(m, h):
+            weigh_direct(m, h, 0, 256)
+            weigh_direct(m, h, 256, 512)
+            add_up(m, h, 0, 256)
+            add_up(m, h, 256, 512)
+            store(m, h, 0, 512)
 
-        def take_x(m):
-            copy_x(m, 0, vcopy)
-            copy_x(m, 1, scopy)
-            copy_x(m, 2, vcopy)
-            for s in range(3):
-                quantize_x(m, s)
+        def far_passes(chunks):
+            for m, g in chunks:
+                for h in range(H):
+                    one_pass("far", m, h, g)
 
-        product("far", 0, 0)
-        reorder_x(1, vcopy)
-        bring_x(1)
-        take_x(1)
-        product("far", 0, 1)
-        keep_far(0, 0)
-        product("far", 1, 0)
-        reorder_x(2, scopy)
-        keep_far(0, 1)
-        bring_x(2)
-        take_x(2)
-        product("far", 1, 1)
-        reorder_x(3, scopy)
-        reorder_x(4, vcopy)
-        copy_d(0, 0, vcopy)
-        keep_far(1, 0)
-        product("far", 2, 0)
-        keep_far(1, 1)
-        bring_x(3)
-        take_x(3)
-        bring_x(4)
-        take_x(4)
-        product("far", 2, 1)
-        keep_far(2, 0)
-        quantize_d(0, 0)
-        product("far", 3, 0)
-        keep_far(2, 1)
-        copy_d(1, 0, scopy)
-        copy_d(2, 0, vcopy)
-        product("far", 3, 1)
-        keep_far(3, 0)
-        quantize_d(1, 0)
-        quantize_d(2, 0)
-        product("far", 4, 0)
-        keep_far(3, 1)
-        copy_d(3, 0, scopy)
-        product("far", 4, 1)
-        keep_far(4, 0)
-        copy_d(4, 0, vcopy)
+        def spans(m):
+            return [[(m, 0), (m, 1)], [(m, 2), (m, 3)], [(m, 4)]]
 
-        steps = [(kind, m, h) for h in range(H) for kind in ("walk", "direct") for m in range(MT)]
-        last = len(steps) - 1
-        scalar_parts = {3: (1, 0), 4: (1, 1), 6: (2, 0), 7: (2, 1), 8: (3, 0), 9: (3, 1), 10: (4, 0), 11: (4, 1)}
-        vector_chunks = {1: (0, 1)}
-        quantize_at = {0: [(3, 0)], 1: [(4, 0)], 2: [(0, 1)], 6: [(1, 1)], 9: [(2, 1)], 11: [(3, 1)], 13: [(4, 1)]}
-        for s, (kind, m, h) in enumerate(steps):
-            if s < last:
-                product(kind, m, h)
+        def whole(m):
+            return [(m, g) for g in range(G)]
+
+        def turn(m, banks):
+            s = spans(m)
+            for c, b in zip(s, banks):
+                transpose_x(c, b)
+            copy_x(s[0], vcopy)
+            copy_x(s[1], scopy)
+            copy_x(s[2], vcopy)
+            for c in s:
+                quantize_x(c)
+
+        transpose_x([(0, 0)], 6)
+        transpose_x([(1, 0)], 7)
+        for m in range(3):
+            for h in range(H):
+                acc["far", m, h, 0] = psum.tile([P, NH], F32, name="bank%d" % (2 * m + h))
+        copy_x([(0, 0)], vcopy)
+        copy_x([(1, 0)], scopy)
+        quantize_x([(0, 0)])
+        transpose_x([(2, 0)], 6)
+        quantize_x([(1, 0)])
+        copy_x([(2, 0)], scopy)
+        far_passes([(0, 0)])
+        pieces = [[(m, g), (m, g + 1)] for g in (1, 3) for m in range(3)]
+        transpose_x(pieces[0], 7)
+        quantize_x([(2, 0)])
+        copy_x(pieces[0], scopy)
+        far_passes([(1, 0), (2, 0)])
+        for i in range(1, len(pieces)):
+            transpose_x(pieces[i], 7 - i % 2)
+            quantize_x(pieces[i - 1])
+            copy_x(pieces[i], scopy)
+            if i + 1 < len(pieces):
+                reorder_x(pieces[i + 1], vcopy)
             else:
-                product(kind, m, h, 0, 256)
-                product(kind, m, h, 256, 512)
-            if s == 0:
-                keep_far(4, 1)
-            elif steps[s - 1][0] == "walk":
-                restart(*steps[s - 1][1:])
-            if s in vector_chunks:
-                copy_d(*vector_chunks[s], vcopy)
-            if s in scalar_parts:
-                g, part = scalar_parts[s]
-                copy_d(g, 1, scopy, 256 * part, 256 * (part + 1))
-            for chunk in quantize_at.get(s, []):
-                quantize_d(*chunk)
-            if s >= 2:
-                before, mb, hb = steps[s - 2]
-                if before == "walk":
-                    weigh_far(mb, hb)
-                else:
-                    add_up(mb, hb)
-            if s >= 1 and steps[s - 1][0] == "direct":
-                weigh_direct(*steps[s - 1][1:])
+                reorder_x(whole(3), vcopy)
+            far_passes(pieces[i - 1])
+            if i == 4:
+                keep_far(0, 0)
+            if i == 5:
+                keep_far(0, 1)
+        quantize_x(pieces[-1])
+        turn(3, (7, 0, 1))
+        keep_far(1, 0)
+        keep_far(1, 1)
+        reorder_x(whole(4), vcopy)
+        copy_d(0, 0, vcopy)
+        far_passes(pieces[-1])
+        product("far", 3, 0, 6)
+        keep_far(2, 0)
+        turn(4, (2, 3, 7))
+        keep_far(2, 1)
+        quantize_d(0, 0)
+        copy_d(1, 0, vcopy)
+
+        steps = [("far", 3, 1), ("far", 4, 0), ("far", 4, 1)]
+        steps = steps + [(kind, m, h) for h in range(H) for kind in ("walk", "direct") for m in range(MT)]
+        last = len(steps) - 1
+        scalar_units = [(2, 0), (4, 0), (0, 1), (1, 1), (2, 1), (3, 1)]
+        scalar_parts = [(g, h, c) for g, h in scalar_units for c in (0, 256)]
+        scalar_at = dict(zip((0, 1, 3, 4, 5, 6, 8, 9, 10, 11, 12, 13), scalar_parts))
+        vector_at = {2: (3, 0), 14: (4, 1)}
+        quantize_at = {1: (1, 0), 2: (2, 0), 3: (3, 0), 6: (4, 0), 8: (0, 1), 11: (1, 1), 14: (2, 1), 15: (3, 1), 16: (4, 1)}
+        before = ("far", 3, 0)
+        for s, (kind, m, h) in enumerate(steps):
+            bank = s % 8
+            if s < last:
+                product(kind, m, h, bank)
+            else:
+                product(kind, m, h, bank, 0, 256)
+                product(kind, m, h, (bank + 1) % 8, 256, 384)
+                product(kind, m, h, (bank + 2) % 8, 384, 512)
+            if before[0] == "far":
+                keep_far(*before[1:])
+            if before[0] == "walk":
+                restart(*before[1:])
+            if s in scalar_at:
+                g, hh, c = scalar_at[s]
+                copy_d(g, hh, scopy, c, c + 256)
+            if s in quantize_at:
+                quantize_d(*quantize_at[s])
+            if s in vector_at:
+                copy_d(*vector_at[s], vcopy)
+            if s >= 2 and steps[s - 2][0] == "walk":
+                weigh_far(*steps[s - 2][1:])
+            if before[0] == "direct":
+                finish(before[1], before[2])
+            before = (kind, m, h)
         m, h = steps[last][1:]
-        weigh_direct(m, h, 0, 256)
-        add_up(m - 1, h)
-        weigh_direct(m, h, 256, 512)
+        weigh_direct(m, h, 0, 256, 0)
+        weigh_direct(m, h, 256, 384, 256)
         add_up(m, h, 0, 256)
-        add_up(m, h, 256, 512)
+        store(m, h, 0, 256)
+        weigh_direct(m, h, 384, 512, 384)
+        add_up(m, h, 256, 384)
+        add_up(m, h, 384, 512)
+        store(m, h, 256, 512)

@@ -22,7 +22,6 @@ G = K // 512
 MT = D // P
 NH = 512
 H = N // NH
-RUNS = [(0, 1), (1, 3), (3, 5)]
 
 
 def tile_drug_restart_scores_s10_kernel(
@@ -38,10 +37,8 @@ def tile_drug_restart_scores_s10_kernel(
         scopy = nc.scalar.copy
 
         ident = keep.tile([P, P], F32, name="ident", align_bytes=256)
-        x_codes = [keep.tile([P, G, P], U32, name="x_codes%d" % m, align_bytes=256) for m in range(MT)]
-        x_scales = [keep.tile([P, G, P], U8, name="x_scales%d" % m, align_bytes=256) for m in range(MT)]
         f_words = [keep.tile([P, 2 * N], U8, name="f_words%d" % g, align_bytes=256) for g in range(G)]
-        f_scales = {g0: keep.tile([P, g1 - g0, N], U8, name="f_scales%d" % g0, align_bytes=256) for g0, g1 in RUNS}
+        f_scales = keep.tile([P, G, N], U8, name="f_scales", align_bytes=256)
         w_words = [keep.tile([P, G, NH], U32, name="w_words%d" % h, align_bytes=256) for h in range(H)]
         w_scales = [keep.tile([P, N], U8, name="w_scales%d" % i, align_bytes=256) for i in range(2)]
         d_raw = [[keep.tile([P, 4, NH], BF16, name="d_raw%d%d" % (g, h), align_bytes=256) for h in range(H)] for g in range(G)]
@@ -53,14 +50,9 @@ def tile_drug_restart_scores_s10_kernel(
 
         x_raw = {}
 
-        def load_x(m0, m1, g0, g1):
-            t = keep.tile([P, m1 - m0, 512 * (g1 - g0)], BF16, name="x_raw%d%d" % (m0, g0), align_bytes=256)
-            rows = seeds[m0 * P : m1 * P, 512 * g0 : 512 * g1]
-            nc.sync.dma_start(out=t[:], in_=rows.rearrange("(m p) k -> p m k", p=P))
-            words = t[:].rearrange("p m k -> p (m k)").bitcast(F32)
-            for m in range(m0, m1):
-                for g in range(g0, g1):
-                    x_raw[m, g] = (words, 256 * ((m - m0) * (g1 - g0) + g - g0))
+        def load_x(m):
+            x_raw[m] = keep.tile([P, K], BF16, name="x_raw%d" % m, align_bytes=256)
+            nc.sync.dma_start(out=x_raw[m][:], in_=seeds[m * P : (m + 1) * P, :])
 
         def load_far(g):
             nc.sync.dma_start(out=f_words[g][:].bitcast(I32), in_=far_words.bitcast(I32)[g])
@@ -72,11 +64,11 @@ def tile_drug_restart_scores_s10_kernel(
                 in_=words[g0:g1, :, h * NH : (h + 1) * NH].rearrange("g p w -> p g w"),
             )
 
-        def load_far_scales(g0, g1):
+        def load_far_scales():
             for r in range(4):
                 nc.sync.dma_start(
-                    out=f_scales[g0][:].bitcast(I32)[r:P:32, :, :],
-                    in_=far_scales.bitcast(I32)[g0:g1, r:16:4, :].rearrange("g q w -> q g w"),
+                    out=f_scales[:].bitcast(I32)[r:P:32, :, :],
+                    in_=far_scales.bitcast(I32)[:, r:16:4, :].rearrange("g q w -> q g w"),
                 )
 
         def load_walk_scales_packed():
@@ -96,89 +88,74 @@ def tile_drug_restart_scores_s10_kernel(
             rows = modules[512 * g : 512 * (g + 1), h * NH : (h + 1) * NH]
             nc.sync.dma_start(out=d_raw[g][h][:], in_=rows.rearrange("(p j) w -> p j w", j=4))
 
-        nc.gpsimd.memset(f_scales[0][:].bitcast(I32), 0)
         make_identity(nc, ident[:])
-        nc.vector.memset(f_scales[1][:].bitcast(I32), 0)
-        nc.vector.memset(f_scales[3][:].bitcast(I32), 0)
+        nc.vector.memset(f_scales[:].bitcast(I32), 0)
         nc.vector.memset(w_scales[0][:].bitcast(I32), 0)
         nc.vector.memset(w_scales[1][:].bitcast(I32), 0)
 
-        load_x(0, 2, 0, 1)
-        load_far_scales(0, 1)
+        load_x(0)
+        load_x(1)
+        load_far_scales()
         load_far(0)
-        load_x(2, 3, 0, 1)
-        load_x(0, 1, 1, 3)
-        load_far_scales(1, 3)
         load_far(1)
-        load_x(1, 2, 1, 3)
         load_far(2)
-        load_x(2, 3, 1, 3)
-        load_x(0, 1, 3, 5)
-        load_far_scales(3, 5)
-        load_x(1, 2, 3, 5)
+        load_x(2)
         load_far(3)
-        load_x(2, 3, 3, 5)
         load_far(4)
-        load_x(3, 4, 0, 5)
+        load_x(3)
+        load_x(4)
         load_modules(0, 0)
-        load_x(4, 5, 0, 5)
         load_walk_scales_packed()
         load_walk_scales_last()
         load_modules(1, 0)
-        load_modules(2, 0)
         load_walk(0, 5, 0)
+        load_modules(2, 0)
         load_modules(3, 0)
         load_modules(4, 0)
         load_modules(0, 1)
+        load_walk(0, 5, 1)
         load_modules(1, 1)
         load_modules(2, 1)
-        load_walk(0, 5, 1)
         load_modules(3, 1)
         load_modules(4, 1)
 
         ordered = {}
         turned = {}
         grouped = {}
+        x_operands = {}
 
-        def reorder_x(chunks, engine_copy):
-            n = len(chunks)
-            t = stage.tile([P, n, 2, P], F32, name="x_ordered%d" % n, align_bytes=256)
-            words, w0 = x_raw[chunks[0]]
-            engine_copy(out=t[:], in_=words[:, w0 : w0 + 256 * n].rearrange("r (c p u) -> r c u p", u=2, p=P))
-            for i, c in enumerate(chunks):
-                ordered[c] = (t, i)
+        def reorder_x(m, engine_copy):
+            ordered[m] = stage.tile([P, G, 2, P], F32, name="x_ordered", align_bytes=256)
+            engine_copy(out=ordered[m][:], in_=x_raw[m][:].bitcast(F32).rearrange("r (g p u) -> r g u p", u=2, p=P))
 
-        def transpose_x(chunks, b):
+        def transpose_x(piece, b):
             bank = psum.tile([P, 2, 2, P], F32, name="bank%d" % b)
-            for j, c in enumerate(chunks):
+            for j, (m, g) in enumerate(piece):
                 for u in range(2):
-                    if c in ordered:
-                        t, i = ordered[c]
-                        src = t[:, i, u, :]
+                    if m in ordered:
+                        src = ordered[m][:, g, u, :]
                     else:
-                        words, w0 = x_raw[c]
-                        src = words[:, w0 + u : w0 + 256 : 2]
+                        src = x_raw[m][:].bitcast(F32)[:, 256 * g + u : 256 * (g + 1) : 2]
                     nc.tensor.transpose(bank[:, j, u, :], src, ident[:])
-            turned[chunks[0]] = bank
+            turned[piece] = bank
 
-        def copy_x(chunks, engine_copy):
-            n = len(chunks)
+        def copy_x(piece, engine_copy):
+            n = len(piece)
             t = stage.tile([P, 2, P, 4], BF16, name="x_grouped", align_bytes=256, bufs=4)
-            engine_copy(out=t[:].bitcast(F32)[:, 0:n], in_=turned[chunks[0]][:, 0:n, :, :].rearrange("p c u r -> p c r u"))
-            grouped[chunks[0]] = t
+            engine_copy(out=t[:].bitcast(F32)[:, 0:n], in_=turned[piece][:, 0:n, :, :].rearrange("p c u r -> p c r u"))
+            grouped[piece] = t
 
-        def x_operand(m, g):
-            return x_codes[m][:, g, :], x_scales[m][:, g, :]
-
-        def quantize_x(chunks):
-            n = len(chunks)
-            m, g = chunks[0]
-            codes, scales = x_codes[m][:, g : g + n, :], x_scales[m][:, g : g + n, :]
+        def quantize_x(piece):
+            n = len(piece)
+            codes = keep.tile([P, n * P], U32, name="x_codes%d%d" % piece[0], align_bytes=256)
+            scales = keep.tile([P, n * P], U8, name="x_scales%d%d" % piece[0], align_bytes=256)
             nc.vector.quantize_mx(
-                out=codes.rearrange("p c r -> p (c r)").bitcast(E4M3),
-                scales=scales.rearrange("p c r -> p (c r)"),
-                in_=grouped[chunks[0]][:, 0:n].rearrange("p c r j -> p (c r j)"),
+                out=codes[:].bitcast(E4M3),
+                scales=scales[:],
+                in_=grouped[piece][:, 0:n].rearrange("p c r j -> p (c r j)"),
             )
+            for j, chunk in enumerate(piece):
+                x_operands[chunk] = (codes[:, j * P : (j + 1) * P], scales[:, j * P : (j + 1) * P])
 
         d_grouped = {}
 
@@ -203,14 +180,13 @@ def tile_drug_restart_scores_s10_kernel(
         def one_pass(kind, m, h, g, c0=0, c1=NH):
             n0, n1 = h * NH + c0, h * NH + c1
             if kind == "far":
-                g0 = max(a for a, b in RUNS if a <= g)
-                rhs, scale = f_words[g][:, 2 * n0 : 2 * n1].bitcast(E2M1), f_scales[g0][:, g - g0, n0:n1]
+                rhs, scale = f_words[g][:, 2 * n0 : 2 * n1].bitcast(E2M1), f_scales[:, g, n0:n1]
             elif kind == "walk":
                 rhs = w_words[h][:, g, c0:c1].bitcast(E4M3)
                 scale = w_scales[g // 4][4 * (g % 4) :, n0:n1]
             else:
                 rhs, scale = d_codes[:, g, n0:n1].bitcast(E4M3), d_scales[:, g, n0:n1]
-            codes, scales = x_operand(m, g)
+            codes, scales = x_operands[m, g]
             nc.tensor.matmul_mx(
                 out=acc[kind, m, h, c0][:, c0:c1],
                 lhsT=codes.bitcast(E4M3),
@@ -259,82 +235,77 @@ def tile_drug_restart_scores_s10_kernel(
             add_up(m, h, 256, 512)
             store(m, h, 0, 512)
 
-        def far_passes(chunks):
-            for m, g in chunks:
+        def far_passes(g):
+            for m in range(2):
                 for h in range(H):
                     one_pass("far", m, h, g)
 
-        def spans(m):
-            return [[(m, 0), (m, 1)], [(m, 2), (m, 3)], [(m, 4)]]
+        def pieces(ma, mb):
+            return [((ma, 0), (ma, 1)), ((ma, 2), (ma, 3)), ((mb, 0), (mb, 1)), ((mb, 2), (mb, 3)), ((ma, 4), (mb, 4))]
 
-        def whole(m):
-            return [(m, g) for g in range(G)]
+        def take(group):
+            for i, piece in enumerate(group):
+                copy_x(piece, (vcopy, scopy)[i % 2])
+                if i >= 1:
+                    quantize_x(group[i - 1])
+            quantize_x(group[-1])
 
-        def turn(m, banks):
-            s = spans(m)
-            for c, b in zip(s, banks):
-                transpose_x(c, b)
-            copy_x(s[0], vcopy)
-            copy_x(s[1], scopy)
-            copy_x(s[2], vcopy)
-            for c in s:
-                quantize_x(c)
-
-        transpose_x([(0, 0)], 6)
-        transpose_x([(1, 0)], 7)
-        for m in range(3):
+        first = pieces(0, 1)
+        transpose_x(first[0], 4)
+        transpose_x(first[1], 5)
+        transpose_x(first[2], 6)
+        transpose_x(first[3], 7)
+        copy_x(first[0], vcopy)
+        copy_x(first[1], scopy)
+        transpose_x(first[4], 4)
+        quantize_x(first[0])
+        copy_x(first[2], vcopy)
+        copy_x(first[3], scopy)
+        quantize_x(first[2])
+        quantize_x(first[1])
+        copy_x(first[4], scopy)
+        quantize_x(first[3])
+        quantize_x(first[4])
+        for m in range(2):
             for h in range(H):
                 acc["far", m, h, 0] = psum.tile([P, NH], F32, name="bank%d" % (2 * m + h))
-        copy_x([(0, 0)], vcopy)
-        copy_x([(1, 0)], scopy)
-        quantize_x([(0, 0)])
-        transpose_x([(2, 0)], 6)
-        quantize_x([(1, 0)])
-        copy_x([(2, 0)], scopy)
-        far_passes([(0, 0)])
-        pieces = [[(m, g), (m, g + 1)] for g in (1, 3) for m in range(3)]
-        transpose_x(pieces[0], 7)
-        quantize_x([(2, 0)])
-        copy_x(pieces[0], scopy)
-        far_passes([(1, 0), (2, 0)])
-        for i in range(1, len(pieces)):
-            transpose_x(pieces[i], 7 - i % 2)
-            quantize_x(pieces[i - 1])
-            copy_x(pieces[i], scopy)
-            if i + 1 < len(pieces):
-                reorder_x(pieces[i + 1], vcopy)
-            else:
-                reorder_x(whole(3), vcopy)
-            far_passes(pieces[i - 1])
-            if i == 4:
-                keep_far(0, 0)
-            if i == 5:
-                keep_far(0, 1)
-        quantize_x(pieces[-1])
-        turn(3, (7, 0, 1))
+        reorder_x(2, vcopy)
+        for g in range(G - 1):
+            far_passes(g)
+        third = [((2, 0), (2, 1)), ((2, 2), (2, 3)), ((2, 4),)]
+        for piece, b in zip(third, (5, 6, 7)):
+            transpose_x(piece, b)
+        reorder_x(3, vcopy)
+        take(third)
+        far_passes(G - 1)
+        reorder_x(4, vcopy)
+        keep_far(0, 0)
+        keep_far(0, 1)
+        product("far", 2, 0, 4)
+        rest = pieces(3, 4)
+        rest = [rest[0], rest[1], rest[4], rest[2], rest[3]]
+        for piece, b in zip(rest, (5, 6, 7, 0, 1)):
+            transpose_x(piece, b)
         keep_far(1, 0)
+        take(rest)
         keep_far(1, 1)
-        reorder_x(whole(4), vcopy)
-        copy_d(0, 0, vcopy)
-        far_passes(pieces[-1])
-        product("far", 3, 0, 6)
+        product("far", 2, 1, 2)
         keep_far(2, 0)
-        turn(4, (2, 3, 7))
+        product("far", 3, 0, 3)
         keep_far(2, 1)
-        quantize_d(0, 0)
-        copy_d(1, 0, vcopy)
+        copy_d(0, 0, vcopy)
 
         steps = [("far", 3, 1), ("far", 4, 0), ("far", 4, 1)]
         steps = steps + [(kind, m, h) for h in range(H) for kind in ("walk", "direct") for m in range(MT)]
         last = len(steps) - 1
         scalar_units = [(2, 0), (4, 0), (0, 1), (1, 1), (2, 1), (3, 1)]
         scalar_parts = [(g, h, c) for g, h in scalar_units for c in (0, 256)]
-        scalar_at = dict(zip((0, 1, 3, 4, 5, 6, 8, 9, 10, 11, 12, 13), scalar_parts))
-        vector_at = {2: (3, 0), 14: (4, 1)}
-        quantize_at = {1: (1, 0), 2: (2, 0), 3: (3, 0), 6: (4, 0), 8: (0, 1), 11: (1, 1), 14: (2, 1), 15: (3, 1), 16: (4, 1)}
+        scalar_at = dict(zip((1, 2, 3, 4, 5, 6, 8, 9, 10, 11, 12, 13), scalar_parts))
+        vector_at = {0: (1, 0), 2: (3, 0), 14: (4, 1)}
+        quantize_at = {0: (0, 0), 1: (1, 0), 3: (2, 0), 4: (3, 0), 5: (4, 0), 8: (0, 1), 11: (1, 1), 14: (2, 1), 15: (3, 1), 16: (4, 1)}
         before = ("far", 3, 0)
         for s, (kind, m, h) in enumerate(steps):
-            bank = s % 8
+            bank = (4 + s) % 8
             if s < last:
                 product(kind, m, h, bank)
             else:

@@ -99,8 +99,8 @@ def tile_drug_restart_scores_s10_kernel(
         load_far(0)
         load_far(1)
         load_far(2)
-        load_x(2)
         load_far(3)
+        load_x(2)
         load_far(4)
         load_x(3)
         load_x(4)
@@ -113,27 +113,33 @@ def tile_drug_restart_scores_s10_kernel(
         load_modules(3, 0)
         load_modules(4, 0)
         load_modules(0, 1)
-        load_walk(0, 5, 1)
         load_modules(1, 1)
         load_modules(2, 1)
+        load_walk(0, 5, 1)
         load_modules(3, 1)
         load_modules(4, 1)
 
         ordered = {}
+        sorted_words = {}
         turned = {}
         grouped = {}
         x_operands = {}
 
-        def reorder_x(m, engine_copy):
-            ordered[m] = stage.tile([P, G, 2, P], F32, name="x_ordered", align_bytes=256)
-            engine_copy(out=ordered[m][:], in_=x_raw[m][:].bitcast(F32).rearrange("r (g p u) -> r g u p", u=2, p=P))
+        def reorder_x(m, g0, g1, engine_copy):
+            if m not in sorted_words:
+                sorted_words[m] = stage.tile([P, 2, G * P], F32, name="x_ordered", align_bytes=256)
+            t = sorted_words[m]
+            words = x_raw[m][:].bitcast(F32)[:, 256 * g0 : 256 * g1]
+            engine_copy(out=t[:, :, P * g0 : P * g1], in_=words.rearrange("r (w u) -> r u w", u=2))
+            for g in range(g0, g1):
+                ordered[m, g] = t[:, :, P * g : P * (g + 1)]
 
         def transpose_x(piece, b):
             bank = psum.tile([P, 2, 2, P], F32, name="bank%d" % b)
             for j, (m, g) in enumerate(piece):
                 for u in range(2):
-                    if m in ordered:
-                        src = ordered[m][:, g, u, :]
+                    if (m, g) in ordered:
+                        src = ordered[m, g][:, u, :]
                     else:
                         src = x_raw[m][:].bitcast(F32)[:, 256 * g + u : 256 * (g + 1) : 2]
                     nc.tensor.transpose(bank[:, j, u, :], src, ident[:])
@@ -235,10 +241,9 @@ def tile_drug_restart_scores_s10_kernel(
             add_up(m, h, 256, 512)
             store(m, h, 0, 512)
 
-        def far_passes(g):
-            for m in range(2):
-                for h in range(H):
-                    one_pass("far", m, h, g)
+        def far_passes(m, g):
+            for h in range(H):
+                one_pass("far", m, h, g)
 
         def pieces(ma, mb):
             return [((ma, 0), (ma, 1)), ((ma, 2), (ma, 3)), ((mb, 0), (mb, 1)), ((mb, 2), (mb, 3)), ((ma, 4), (mb, 4))]
@@ -252,33 +257,37 @@ def tile_drug_restart_scores_s10_kernel(
 
         first = pieces(0, 1)
         transpose_x(first[0], 4)
+        reorder_x(0, 2, 5, vcopy)
         transpose_x(first[1], 5)
+        copy_x(first[0], scopy)
+        reorder_x(1, 0, 2, vcopy)
+        reorder_x(1, 2, 5, vcopy)
         transpose_x(first[2], 6)
         transpose_x(first[3], 7)
-        copy_x(first[0], vcopy)
-        copy_x(first[1], scopy)
         transpose_x(first[4], 4)
+        copy_x(first[1], scopy)
         quantize_x(first[0])
         copy_x(first[2], vcopy)
         copy_x(first[3], scopy)
-        quantize_x(first[2])
         quantize_x(first[1])
+        quantize_x(first[2])
         copy_x(first[4], scopy)
         quantize_x(first[3])
         quantize_x(first[4])
         for m in range(2):
             for h in range(H):
                 acc["far", m, h, 0] = psum.tile([P, NH], F32, name="bank%d" % (2 * m + h))
-        reorder_x(2, vcopy)
-        for g in range(G - 1):
-            far_passes(g)
+        reorder_x(2, 0, 5, vcopy)
+        for m, g in ((0, 0), (0, 1), (1, 0), (1, 1), (0, 2), (1, 2), (0, 3), (1, 3)):
+            far_passes(m, g)
         third = [((2, 0), (2, 1)), ((2, 2), (2, 3)), ((2, 4),)]
         for piece, b in zip(third, (5, 6, 7)):
             transpose_x(piece, b)
-        reorder_x(3, vcopy)
         take(third)
-        far_passes(G - 1)
-        reorder_x(4, vcopy)
+        reorder_x(3, 0, 5, vcopy)
+        far_passes(0, 4)
+        far_passes(1, 4)
+        reorder_x(4, 0, 5, vcopy)
         keep_far(0, 0)
         keep_far(0, 1)
         product("far", 2, 0, 4)
@@ -298,20 +307,18 @@ def tile_drug_restart_scores_s10_kernel(
         steps = [("far", 3, 1), ("far", 4, 0), ("far", 4, 1)]
         steps = steps + [(kind, m, h) for h in range(H) for kind in ("walk", "direct") for m in range(MT)]
         last = len(steps) - 1
-        scalar_units = [(2, 0), (4, 0), (0, 1), (1, 1), (2, 1), (3, 1)]
+        scalar_units = [(3, 0), (0, 1), (1, 1), (2, 1), (3, 1), (4, 1)]
         scalar_parts = [(g, h, c) for g, h in scalar_units for c in (0, 256)]
-        scalar_at = dict(zip((1, 2, 3, 4, 5, 6, 8, 9, 10, 11, 12, 13), scalar_parts))
-        vector_at = {0: (1, 0), 2: (3, 0), 14: (4, 1)}
-        quantize_at = {0: (0, 0), 1: (1, 0), 3: (2, 0), 4: (3, 0), 5: (4, 0), 8: (0, 1), 11: (1, 1), 14: (2, 1), 15: (3, 1), 16: (4, 1)}
+        scalar_at = dict(zip((4, 5, 6, 7, 8, 9, 10, 11, 12, 13, 14, 15), scalar_parts))
+        vector_at = {0: (1, 0), 3: (2, 0), 5: (4, 0)}
+        quantize_at = {0: (0, 0), 1: (1, 0), 4: (2, 0), 6: (3, 0), 7: (4, 0), 13: (0, 1), 14: (1, 1), 15: (2, 1), 16: (3, 1), 17: (4, 1)}
         before = ("far", 3, 0)
         for s, (kind, m, h) in enumerate(steps):
             bank = (4 + s) % 8
-            if s < last:
+            if s < last - 1:
                 product(kind, m, h, bank)
             else:
-                product(kind, m, h, bank, 0, 256)
-                product(kind, m, h, (bank + 1) % 8, 256, 384)
-                product(kind, m, h, (bank + 2) % 8, 384, 512)
+                break
             if before[0] == "far":
                 keep_far(*before[1:])
             if before[0] == "walk":
@@ -328,12 +335,19 @@ def tile_drug_restart_scores_s10_kernel(
             if before[0] == "direct":
                 finish(before[1], before[2])
             before = (kind, m, h)
-        m, h = steps[last][1:]
-        weigh_direct(m, h, 0, 256, 0)
-        weigh_direct(m, h, 256, 384, 256)
-        add_up(m, h, 0, 256)
-        store(m, h, 0, 256)
-        weigh_direct(m, h, 384, 512, 384)
-        add_up(m, h, 256, 384)
-        add_up(m, h, 384, 512)
+        tail = [(MT - 2, 0, 256), (MT - 2, 256, 512), (MT - 1, 0, 256), (MT - 1, 256, 384), (MT - 1, 384, 512)]
+        h = H - 1
+        for i, (m, c0, c1) in enumerate(tail):
+            product("direct", m, h, (bank + i) % 8, c0, c1)
+            if i == 0:
+                finish(MT - 3, h)
+        for i, (m, c0, c1) in enumerate(tail):
+            weigh_direct(m, h, c0, c1, c0)
+            if i >= 1:
+                add_up(tail[i - 1][0], h, tail[i - 1][1], tail[i - 1][2])
+            if i == 2:
+                store(MT - 2, h, 0, 512)
+            if i == 3:
+                store(MT - 1, h, 0, 256)
+        add_up(m, h, c0, c1)
         store(m, h, 256, 512)

@@ -92,6 +92,8 @@ def tile_drug_restart_scores_s10_kernel(
         nc.vector.memset(f_scales[:].bitcast(I32), 0)
         nc.vector.memset(w_scales[0][:].bitcast(I32), 0)
         nc.vector.memset(w_scales[1][:].bitcast(I32), 0)
+        nc.vector.memset(d_codes[:, G - 1, 0:NH], 0)
+        nc.vector.memset(d_scales[:, G - 1, 0:NH].bitcast(I32), 0)
 
         load_x(0)
         load_x(1)
@@ -245,6 +247,19 @@ def tile_drug_restart_scores_s10_kernel(
             for h in range(H):
                 one_pass("far", m, h, g)
 
+        def warm_up(count, b):
+            bank = psum.tile([P, NH], F32, name="bank%d" % b)
+            for i in range(count):
+                nc.tensor.matmul_mx(
+                    out=bank[:],
+                    lhsT=d_codes[:, G - 1, 0:P].bitcast(E4M3),
+                    lhsT_scale=d_scales[:, G - 1, 0:P],
+                    rhs=d_codes[:, G - 1, 0:NH].bitcast(E4M3),
+                    rhs_scale=d_scales[:, G - 1, 0:NH],
+                    start=True,
+                    stop=True,
+                )
+
         def pieces(ma, mb):
             return [((ma, 0), (ma, 1)), ((ma, 2), (ma, 3)), ((mb, 0), (mb, 1)), ((mb, 2), (mb, 3)), ((ma, 4), (mb, 4))]
 
@@ -256,15 +271,18 @@ def tile_drug_restart_scores_s10_kernel(
             quantize_x(group[-1])
 
         first = pieces(0, 1)
+        warm_up(2, 3)
         transpose_x(first[0], 4)
         reorder_x(0, 2, 5, vcopy)
         transpose_x(first[1], 5)
+        warm_up(2, 3)
         copy_x(first[0], scopy)
         reorder_x(1, 0, 2, vcopy)
         reorder_x(1, 2, 5, vcopy)
         transpose_x(first[2], 6)
         transpose_x(first[3], 7)
         transpose_x(first[4], 4)
+        warm_up(2, 3)
         copy_x(first[1], scopy)
         quantize_x(first[0])
         copy_x(first[2], vcopy)

@@ -50,9 +50,11 @@ def tile_drug_restart_scores_s10_kernel(
 
         x_raw = {}
 
-        def load_x(m):
-            x_raw[m] = keep.tile([P, K], BF16, name="x_raw%d" % m, align_bytes=256)
-            nc.sync.dma_start(out=x_raw[m][:], in_=seeds[m * P : (m + 1) * P, :])
+        def load_x(m, g0=0, g1=G):
+            t = keep.tile([P, 512 * (g1 - g0)], BF16, name="x_raw%d%d" % (m, g0), align_bytes=256)
+            nc.sync.dma_start(out=t[:], in_=seeds[m * P : (m + 1) * P, 512 * g0 : 512 * g1])
+            for g in range(g0, g1):
+                x_raw[m, g] = (t, g0)
 
         def load_far(g):
             nc.sync.dma_start(out=f_words[g][:].bitcast(I32), in_=far_words.bitcast(I32)[g])
@@ -90,19 +92,20 @@ def tile_drug_restart_scores_s10_kernel(
 
         make_identity(nc, ident[:])
         nc.vector.memset(f_scales[:].bitcast(I32), 0)
-        nc.vector.memset(w_scales[0][:].bitcast(I32), 0)
-        nc.vector.memset(w_scales[1][:].bitcast(I32), 0)
         nc.vector.memset(d_codes[:, G - 1, 0:NH], 0)
         nc.vector.memset(d_scales[:, G - 1, 0:NH].bitcast(I32), 0)
+        nc.vector.memset(w_scales[0][:].bitcast(I32), 0)
+        nc.vector.memset(w_scales[1][:].bitcast(I32), 0)
 
-        load_x(0)
+        load_x(0, 0, 2)
+        load_x(0, 2, 5)
         load_x(1)
         load_far_scales()
         load_far(0)
         load_far(1)
         load_far(2)
-        load_far(3)
         load_x(2)
+        load_far(3)
         load_far(4)
         load_x(3)
         load_x(4)
@@ -131,7 +134,8 @@ def tile_drug_restart_scores_s10_kernel(
             if m not in sorted_words:
                 sorted_words[m] = stage.tile([P, 2, G * P], F32, name="x_ordered", align_bytes=256)
             t = sorted_words[m]
-            words = x_raw[m][:].bitcast(F32)[:, 256 * g0 : 256 * g1]
+            raw, base = x_raw[m, g0]
+            words = raw[:].bitcast(F32)[:, 256 * (g0 - base) : 256 * (g1 - base)]
             engine_copy(out=t[:, :, P * g0 : P * g1], in_=words.rearrange("r (w u) -> r u w", u=2))
             for g in range(g0, g1):
                 ordered[m, g] = t[:, :, P * g : P * (g + 1)]
@@ -143,7 +147,8 @@ def tile_drug_restart_scores_s10_kernel(
                     if (m, g) in ordered:
                         src = ordered[m, g][:, u, :]
                     else:
-                        src = x_raw[m][:].bitcast(F32)[:, 256 * g + u : 256 * (g + 1) : 2]
+                        raw, base = x_raw[m, g]
+                        src = raw[:].bitcast(F32)[:, 256 * (g - base) + u : 256 * (g - base + 1) : 2]
                     nc.tensor.transpose(bank[:, j, u, :], src, ident[:])
             turned[piece] = bank
 
@@ -271,8 +276,8 @@ def tile_drug_restart_scores_s10_kernel(
             quantize_x(group[-1])
 
         first = pieces(0, 1)
-        warm_up(2, 3)
         transpose_x(first[0], 4)
+        warm_up(3, 3)
         reorder_x(0, 2, 5, vcopy)
         transpose_x(first[1], 5)
         warm_up(2, 3)
@@ -282,7 +287,6 @@ def tile_drug_restart_scores_s10_kernel(
         transpose_x(first[2], 6)
         transpose_x(first[3], 7)
         transpose_x(first[4], 4)
-        warm_up(2, 3)
         copy_x(first[1], scopy)
         quantize_x(first[0])
         copy_x(first[2], vcopy)
@@ -295,41 +299,56 @@ def tile_drug_restart_scores_s10_kernel(
         for m in range(2):
             for h in range(H):
                 acc["far", m, h, 0] = psum.tile([P, NH], F32, name="bank%d" % (2 * m + h))
-        reorder_x(2, 0, 5, vcopy)
-        for m, g in ((0, 0), (0, 1), (1, 0), (1, 1), (0, 2), (1, 2), (0, 3), (1, 3)):
+        reorder_x(2, 0, 2, vcopy)
+        reorder_x(2, 2, 5, vcopy)
+        for m, g in ((0, 0), (0, 1), (0, 2), (1, 0), (1, 1), (1, 2)):
             far_passes(m, g)
         third = [((2, 0), (2, 1)), ((2, 2), (2, 3)), ((2, 4),)]
         for piece, b in zip(third, (5, 6, 7)):
             transpose_x(piece, b)
         take(third)
         reorder_x(3, 0, 5, vcopy)
-        far_passes(0, 4)
-        far_passes(1, 4)
+        for m, g in ((0, 3), (0, 4), (1, 3), (1, 4)):
+            far_passes(m, g)
         reorder_x(4, 0, 5, vcopy)
         keep_far(0, 0)
         keep_far(0, 1)
-        product("far", 2, 0, 4)
-        rest = pieces(3, 4)
-        rest = [rest[0], rest[1], rest[4], rest[2], rest[3]]
-        for piece, b in zip(rest, (5, 6, 7, 0, 1)):
-            transpose_x(piece, b)
         keep_far(1, 0)
-        take(rest)
         keep_far(1, 1)
+        rest = pieces(3, 4)
+        acc["far", 2, 0, 0] = psum.tile([P, NH], F32, name="bank4")
+        for g in range(3):
+            one_pass("far", 2, 0, g)
+        transpose_x(rest[0], 5)
+        transpose_x(rest[1], 6)
+        for g in range(3, G):
+            one_pass("far", 2, 0, g)
+        transpose_x(rest[4], 7)
+        transpose_x(rest[2], 0)
+        transpose_x(rest[3], 1)
+        take([rest[0], rest[1], rest[4], rest[2], rest[3]])
         product("far", 2, 1, 2)
         keep_far(2, 0)
+        copy_d(1, 0, scopy, 0, 256)
         product("far", 3, 0, 3)
-        keep_far(2, 1)
         copy_d(0, 0, vcopy)
+        copy_d(1, 0, scopy, 256, 512)
+        keep_far(2, 1)
 
         steps = [("far", 3, 1), ("far", 4, 0), ("far", 4, 1)]
         steps = steps + [(kind, m, h) for h in range(H) for kind in ("walk", "direct") for m in range(MT)]
         last = len(steps) - 1
-        scalar_units = [(3, 0), (0, 1), (1, 1), (2, 1), (3, 1), (4, 1)]
-        scalar_parts = [(g, h, c) for g, h in scalar_units for c in (0, 256)]
-        scalar_at = dict(zip((4, 5, 6, 7, 8, 9, 10, 11, 12, 13, 14, 15), scalar_parts))
-        vector_at = {0: (1, 0), 3: (2, 0), 5: (4, 0)}
-        quantize_at = {0: (0, 0), 1: (1, 0), 4: (2, 0), 6: (3, 0), 7: (4, 0), 13: (0, 1), 14: (1, 1), 15: (2, 1), 16: (3, 1), 17: (4, 1)}
+        walk0, direct0, walk1 = 3, 3 + MT, 3 + 2 * MT
+        vector_at = {walk0: (2, 0), walk0 + 2: (4, 0), walk1 + 1: (G - 1, 1)}
+        scalar_at = {walk0 + 1: (3, 0, 0), walk0 + 2: (3, 0, 256)}
+        for g in range(G - 1):
+            scalar_at[direct0 + 2 * g] = (g, 1, 0)
+            scalar_at[direct0 + 2 * g + 1] = (g, 1, 256)
+        quantize_at = {0: (0, 0), 1: (1, 0), walk0 + 4: (3, 0), walk1 - 1: (0, 1), walk1: (1, 1), walk1 + 2: (2, 1)}
+        quantize_at[walk0 + 1] = (2, 0)
+        quantize_at[walk0 + 3] = (4, 0)
+        quantize_at[walk1 + 3] = (G - 1, 1)
+        quantize_at[walk1 + 4] = (3, 1)
         before = ("far", 3, 0)
         for s, (kind, m, h) in enumerate(steps):
             bank = (4 + s) % 8
@@ -350,8 +369,13 @@ def tile_drug_restart_scores_s10_kernel(
                 copy_d(*vector_at[s], vcopy)
             if s >= 2 and steps[s - 2][0] == "walk":
                 weigh_far(*steps[s - 2][1:])
-            if before[0] == "direct":
-                finish(before[1], before[2])
+            if before[0] == "direct" and before[2] == 0:
+                weigh_direct(before[1], 0, 0, NH)
+            if s >= 2 and steps[s - 2][0] == "direct" and steps[s - 2][2] == 0:
+                add_up(steps[s - 2][1], 0, 0, NH)
+                store(steps[s - 2][1], 0, 0, NH)
+            if before[0] == "direct" and before[2] == 1:
+                finish(before[1], 1)
             before = (kind, m, h)
         tail = [(MT - 2, 0, 256), (MT - 2, 256, 512), (MT - 1, 0, 256), (MT - 1, 256, 384), (MT - 1, 384, 512)]
         h = H - 1

@@ -106,13 +106,13 @@ def tile_drug_restart_scores_s10_kernel(
         load_far(2)
         load_x(2)
         load_far(3)
-        load_far(4)
         load_x(3)
+        load_far(4)
         load_x(4)
-        load_modules(0, 0)
         load_walk_scales_packed()
-        load_walk_scales_last()
+        load_modules(0, 0)
         load_modules(1, 0)
+        load_walk_scales_last()
         load_walk(0, 5, 0)
         load_modules(2, 0)
         load_modules(3, 0)
@@ -277,13 +277,14 @@ def tile_drug_restart_scores_s10_kernel(
 
         first = pieces(0, 1)
         transpose_x(first[0], 4)
-        warm_up(3, 3)
+        warm_up(2, 3)
         reorder_x(0, 2, 5, vcopy)
         transpose_x(first[1], 5)
         warm_up(2, 3)
         copy_x(first[0], scopy)
         reorder_x(1, 0, 2, vcopy)
-        reorder_x(1, 2, 5, vcopy)
+        reorder_x(1, 4, 5, scopy)
+        reorder_x(1, 2, 4, vcopy)
         transpose_x(first[2], 6)
         transpose_x(first[3], 7)
         transpose_x(first[4], 4)
@@ -300,15 +301,17 @@ def tile_drug_restart_scores_s10_kernel(
             for h in range(H):
                 acc["far", m, h, 0] = psum.tile([P, NH], F32, name="bank%d" % (2 * m + h))
         reorder_x(2, 0, 2, vcopy)
-        reorder_x(2, 2, 5, vcopy)
+        reorder_x(2, 4, 5, scopy)
+        reorder_x(2, 2, 4, vcopy)
         for m, g in ((0, 0), (0, 1), (0, 2), (1, 0), (1, 1), (1, 2)):
             far_passes(m, g)
         third = [((2, 0), (2, 1)), ((2, 2), (2, 3)), ((2, 4),)]
         for piece, b in zip(third, (5, 6, 7)):
             transpose_x(piece, b)
         take(third)
-        reorder_x(3, 0, 5, vcopy)
-        for m, g in ((0, 3), (0, 4), (1, 3), (1, 4)):
+        reorder_x(3, 0, 2, scopy)
+        reorder_x(3, 2, 5, vcopy)
+        for m, g in ((0, 3), (1, 3), (0, 4), (1, 4)):
             far_passes(m, g)
         reorder_x(4, 0, 5, vcopy)
         keep_far(0, 0)
@@ -335,27 +338,26 @@ def tile_drug_restart_scores_s10_kernel(
         copy_d(1, 0, scopy, 256, 512)
         keep_far(2, 1)
 
-        steps = [("far", 3, 1), ("far", 4, 0), ("far", 4, 1)]
+        steps = [("far", 3, 1), ("far", 4, 0)]
         steps = steps + [(kind, m, h) for h in range(H) for kind in ("walk", "direct") for m in range(MT)]
         last = len(steps) - 1
-        walk0, direct0, walk1 = 3, 3 + MT, 3 + 2 * MT
+        walk0, direct0, walk1 = 2, 2 + MT, 2 + 2 * MT
         vector_at = {walk0: (2, 0), walk0 + 2: (4, 0), walk1 + 1: (G - 1, 1)}
         scalar_at = {walk0 + 1: (3, 0, 0), walk0 + 2: (3, 0, 256)}
         for g in range(G - 1):
             scalar_at[direct0 + 2 * g] = (g, 1, 0)
             scalar_at[direct0 + 2 * g + 1] = (g, 1, 256)
-        quantize_at = {0: (0, 0), 1: (1, 0), walk0 + 4: (3, 0), walk1 - 1: (0, 1), walk1: (1, 1), walk1 + 2: (2, 1)}
+        quantize_at = {0: (0, 0), 1: (1, 0), walk0 + 3: (3, 0), walk1 - 1: (0, 1), walk1: (1, 1), walk1 + 2: (2, 1)}
         quantize_at[walk0 + 1] = (2, 0)
-        quantize_at[walk0 + 3] = (4, 0)
+        quantize_at[walk0 + 4] = (4, 0)
         quantize_at[walk1 + 3] = (G - 1, 1)
         quantize_at[walk1 + 4] = (3, 1)
         before = ("far", 3, 0)
         for s, (kind, m, h) in enumerate(steps):
             bank = (4 + s) % 8
-            if s < last - 1:
-                product(kind, m, h, bank)
-            else:
+            if s == last:
                 break
+            product(kind, m, h, bank)
             if before[0] == "far":
                 keep_far(*before[1:])
             if before[0] == "walk":
@@ -367,7 +369,7 @@ def tile_drug_restart_scores_s10_kernel(
                 quantize_d(*quantize_at[s])
             if s in vector_at:
                 copy_d(*vector_at[s], vcopy)
-            if s >= 2 and steps[s - 2][0] == "walk":
+            if s >= 2 and steps[s - 2][0] == "walk" and steps[s - 2][1:] != (MT - 1, H - 1):
                 weigh_far(*steps[s - 2][1:])
             if before[0] == "direct" and before[2] == 0:
                 weigh_direct(before[1], 0, 0, NH)
@@ -377,19 +379,33 @@ def tile_drug_restart_scores_s10_kernel(
             if before[0] == "direct" and before[2] == 1:
                 finish(before[1], 1)
             before = (kind, m, h)
-        tail = [(MT - 2, 0, 256), (MT - 2, 256, 512), (MT - 1, 0, 256), (MT - 1, 256, 384), (MT - 1, 384, 512)]
-        h = H - 1
-        for i, (m, c0, c1) in enumerate(tail):
-            product("direct", m, h, (bank + i) % 8, c0, c1)
-            if i == 0:
-                finish(MT - 3, h)
-        for i, (m, c0, c1) in enumerate(tail):
-            weigh_direct(m, h, c0, c1, c0)
-            if i >= 1:
-                add_up(tail[i - 1][0], h, tail[i - 1][1], tail[i - 1][2])
-            if i == 2:
-                store(MT - 2, h, 0, 512)
-            if i == 3:
-                store(MT - 1, h, 0, 256)
-        add_up(m, h, c0, c1)
-        store(m, h, 256, 512)
+        m, h = MT - 1, H - 1
+        r = r_sb[m, h]
+        nc.scalar.activation(out=r[:], in_=r[:], func=COPY, scale=-0.5, bias=0.5)
+        product("far", m, h, bank)
+        finish(m - 1, h)
+        tail = [(0, 256), (256, 384), (384, 512)]
+        for i, (c0, c1) in enumerate(tail):
+            product("direct", m, h, (bank + 1 + i) % 8, c0, c1)
+        nc.vector.scalar_tensor_tensor(
+            out=f_sb[m, h][:], in0=r[:], scalar=1.0, in1=acc["far", m, h, 0][:], op0=ALU.subtract, op1=ALU.mult
+        )
+        weighed = f_sb[0, 0]
+
+        def last_weigh(c0, c1):
+            nc.vector.tensor_tensor(
+                out=weighed[:, c0:c1], in0=acc["direct", m, h, c0][:, c0:c1], in1=r[:, c0:c1], op=ALU.mult
+            )
+
+        def last_add(c0, c1):
+            nc.vector.tensor_tensor(out=r[:, c0:c1], in0=weighed[:, c0:c1], in1=f_sb[m, h][:, c0:c1], op=ALU.subtract)
+
+        last_weigh(*tail[0])
+        last_weigh(*tail[1])
+        last_add(*tail[0])
+        store(m, h, *tail[0])
+        last_weigh(*tail[2])
+        last_add(*tail[1])
+        store(m, h, *tail[1])
+        last_add(*tail[2])
+        store(m, h, *tail[2])

@@ -38,8 +38,9 @@ def tile_drug_restart_scores_s10_kernel(
 
         ident = keep.tile([P, P], F32, name="ident", align_bytes=256)
         f_words = [keep.tile([P, 2 * N], U8, name="f_words%d" % g, align_bytes=256) for g in range(G)]
-        f_scales = keep.tile([P, G, N], U8, name="f_scales", align_bytes=256)
-        w_words = [keep.tile([P, G, NH], U32, name="w_words%d" % h, align_bytes=256) for h in range(H)]
+        f_runs = [(0, 3), (3, G)]
+        f_scales = [keep.tile([P, g1 - g0, N], U8, name="f_scales%d" % g0, align_bytes=256) for g0, g1 in f_runs]
+        w_words = {}
         w_scales = [keep.tile([P, N], U8, name="w_scales%d" % i, align_bytes=256) for i in range(2)]
         d_raw = [[keep.tile([P, 4, NH], BF16, name="d_raw%d%d" % (g, h), align_bytes=256) for h in range(H)] for g in range(G)]
         d_codes = keep.tile([P, G, N], U32, name="d_codes", align_bytes=256)
@@ -49,6 +50,7 @@ def tile_drug_restart_scores_s10_kernel(
         r_sb = {mh: keep.tile([P, NH], F32, name="r_sb%d%d" % mh, align_bytes=256) for mh in pairs}
 
         x_raw = {}
+        x_quads = {}
 
         def load_x(m, g0=0, g1=G):
             t = keep.tile([P, 512 * (g1 - g0)], BF16, name="x_raw%d%d" % (m, g0), align_bytes=256)
@@ -56,21 +58,33 @@ def tile_drug_restart_scores_s10_kernel(
             for g in range(g0, g1):
                 x_raw[m, g] = (t, g0)
 
+        def load_x_quadrants(m):
+            for b in range(2):
+                t = keep.tile([P, 2 * G, P], BF16, name="x_quads%d%d" % (m, b), align_bytes=256)
+                rows = seeds[m * P + 64 * b : m * P + 64 * (b + 1), :].rearrange("(i e) k -> i (e k)", e=2)
+                runs = rows.rearrange("i (j a c) -> i j a c", a=4, c=P)
+                for a in (0, 2, 1, 3):
+                    nc.sync.dma_start(out=t[32 * a : 32 * (a + 1), :, :], in_=runs[:, :, a, :])
+                x_quads[m, b] = t
+
         def load_far(g):
             nc.sync.dma_start(out=f_words[g][:].bitcast(I32), in_=far_words.bitcast(I32)[g])
 
         def load_walk(g0, g1, h):
+            t = keep.tile([P, g1 - g0, NH], U32, name="w_words%d%d" % (g0, h), align_bytes=256)
             words = walk_words.rearrange("g p n t -> g p (n t)").bitcast(I32)
             nc.sync.dma_start(
-                out=w_words[h][:].bitcast(I32)[:, g0:g1, :],
-                in_=words[g0:g1, :, h * NH : (h + 1) * NH].rearrange("g p w -> p g w"),
+                out=t[:].bitcast(I32), in_=words[g0:g1, :, h * NH : (h + 1) * NH].rearrange("g p w -> p g w")
             )
+            for g in range(g0, g1):
+                w_words[g, h] = t[:, g - g0, :]
 
-        def load_far_scales():
+        def load_far_scales(i):
+            g0, g1 = f_runs[i]
             for r in range(4):
                 nc.sync.dma_start(
-                    out=f_scales[:].bitcast(I32)[r:P:32, :, :],
-                    in_=far_scales.bitcast(I32)[:, r:16:4, :].rearrange("g q w -> q g w"),
+                    out=f_scales[i][:].bitcast(I32)[r:P:32, :, :],
+                    in_=far_scales.bitcast(I32)[g0:g1, r:16:4, :].rearrange("g q w -> q g w"),
                 )
 
         def load_walk_scales_packed():
@@ -91,23 +105,25 @@ def tile_drug_restart_scores_s10_kernel(
             nc.sync.dma_start(out=d_raw[g][h][:], in_=rows.rearrange("(p j) w -> p j w", j=4))
 
         make_identity(nc, ident[:])
-        nc.vector.memset(f_scales[:].bitcast(I32), 0)
-        nc.vector.memset(d_codes[:, G - 1, 0:NH], 0)
-        nc.vector.memset(d_scales[:, G - 1, 0:NH].bitcast(I32), 0)
+        nc.vector.memset(f_scales[0][:].bitcast(I32), 0)
+        nc.vector.memset(f_scales[1][:].bitcast(I32), 0)
         nc.vector.memset(w_scales[0][:].bitcast(I32), 0)
         nc.vector.memset(w_scales[1][:].bitcast(I32), 0)
+        nc.vector.memset(d_codes[:, G - 1, 0:NH], 0)
+        nc.vector.memset(d_scales[:, G - 1, 0:NH].bitcast(I32), 0)
 
         load_x(0, 0, 2)
         load_x(0, 2, 5)
         load_x(1)
-        load_far_scales()
+        load_far_scales(0)
         load_far(0)
         load_far(1)
         load_far(2)
         load_x(2)
+        load_far_scales(1)
         load_far(3)
-        load_x(3)
         load_far(4)
+        load_x(3)
         load_x(4)
         load_walk_scales_packed()
         load_modules(0, 0)
@@ -123,6 +139,7 @@ def tile_drug_restart_scores_s10_kernel(
         load_walk(0, 5, 1)
         load_modules(3, 1)
         load_modules(4, 1)
+
 
         ordered = {}
         sorted_words = {}
@@ -170,6 +187,37 @@ def tile_drug_restart_scores_s10_kernel(
             for j, chunk in enumerate(piece):
                 x_operands[chunk] = (codes[:, j * P : (j + 1) * P], scales[:, j * P : (j + 1) * P])
 
+        v_sorted = {}
+        v_turned = {}
+
+        def sort_quads(m, b, engine_copy):
+            if m not in v_sorted:
+                v_sorted[m] = stage.tile([P, 2, G * P], F32, name="x_ordered", align_bytes=256)
+            t = v_sorted[m][:].rearrange("p u w -> p (u w)").rearrange("p (g b e u w) -> p g b e u w", g=G, b=2, e=2, u=2)
+            words = x_quads[m, b][:].rearrange("p j c -> p (j c)").bitcast(F32)
+            engine_copy(
+                out=t[:, :, b, :, :, :].rearrange("p g e u w -> p e g u w"),
+                in_=words.rearrange("p (e g w u) -> p e g u w", e=2, g=G, u=2),
+            )
+
+        def turn_quads(piece):
+            m, g0 = piece[0]
+            n = len(piece)
+            t = stage.tile([P, 512], F32, name="v_turned", align_bytes=256, bufs=3)
+            flat = v_sorted[m][:].rearrange("p u w -> p (u w)")
+            nc.vector.transpose(t[:, 0 : 256 * n], flat[:, 256 * g0 : 256 * (g0 + n)])
+            v_turned[piece] = t
+
+        def pair_quads(piece, engine_copy):
+            n = len(piece)
+            t = stage.tile([P, 2, P, 4], BF16, name="x_grouped", align_bytes=256, bufs=4)
+            words = t[:].rearrange("p c r j -> p (c r j)").bitcast(F32)[:, 0 : 256 * n]
+            engine_copy(
+                out=words.rearrange("p (c i r) -> p c i r", i=32, r=4),
+                in_=v_turned[piece][:, 0 : 256 * n].rearrange("p (c r i) -> p c i r", i=32, r=4),
+            )
+            grouped[piece] = t
+
         d_grouped = {}
 
         def copy_d(g, h, engine_copy, c0=0, c1=NH):
@@ -193,9 +241,9 @@ def tile_drug_restart_scores_s10_kernel(
         def one_pass(kind, m, h, g, c0=0, c1=NH):
             n0, n1 = h * NH + c0, h * NH + c1
             if kind == "far":
-                rhs, scale = f_words[g][:, 2 * n0 : 2 * n1].bitcast(E2M1), f_scales[:, g, n0:n1]
+                rhs, scale = f_words[g][:, 2 * n0 : 2 * n1].bitcast(E2M1), f_scales[g // 3][:, g % 3, n0:n1]
             elif kind == "walk":
-                rhs = w_words[h][:, g, c0:c1].bitcast(E4M3)
+                rhs = w_words[g, h][:, c0:c1].bitcast(E4M3)
                 scale = w_scales[g // 4][4 * (g % 4) :, n0:n1]
             else:
                 rhs, scale = d_codes[:, g, n0:n1].bitcast(E4M3), d_scales[:, g, n0:n1]
@@ -276,6 +324,7 @@ def tile_drug_restart_scores_s10_kernel(
             quantize_x(group[-1])
 
         first = pieces(0, 1)
+        warm_up(3, 3)
         transpose_x(first[0], 4)
         warm_up(2, 3)
         reorder_x(0, 2, 5, vcopy)

@@ -58,14 +58,12 @@ def tile_drug_restart_scores_s10_kernel(
             for g in range(g0, g1):
                 x_raw[m, g] = (t, g0)
 
-        def load_x_quadrants(m):
-            for b in range(2):
-                t = keep.tile([P, 2 * G, P], BF16, name="x_quads%d%d" % (m, b), align_bytes=256)
-                rows = seeds[m * P + 64 * b : m * P + 64 * (b + 1), :].rearrange("(i e) k -> i (e k)", e=2)
-                runs = rows.rearrange("i (j a c) -> i j a c", a=4, c=P)
-                for a in (0, 2, 1, 3):
-                    nc.sync.dma_start(out=t[32 * a : 32 * (a + 1), :, :], in_=runs[:, :, a, :])
-                x_quads[m, b] = t
+        def load_x_quadrants():
+            t = keep.tile([P, 8, P], BF16, name="x_raw00", align_bytes=256)
+            rows = seeds[3 * P : 5 * P, 512 * (G - 1) :].rearrange("(b i) (a c) -> i b a c", i=32, c=P)
+            for a in (0, 2, 1, 3):
+                nc.sync.dma_start(out=t[32 * a : 32 * (a + 1), :, :], in_=rows[:, :, a, :])
+            x_quads[0] = t
 
         def load_far(g):
             nc.sync.dma_start(out=f_words[g][:].bitcast(I32), in_=far_words.bitcast(I32)[g])
@@ -112,8 +110,8 @@ def tile_drug_restart_scores_s10_kernel(
         nc.vector.memset(d_codes[:, G - 1, 0:NH], 0)
         nc.vector.memset(d_scales[:, G - 1, 0:NH].bitcast(I32), 0)
 
-        load_x(0, 0, 2)
-        load_x(0, 2, 5)
+        load_x(0,0,2)
+        load_x(0,2,5)
         load_x(1)
         load_far_scales(0)
         load_far(0)
@@ -123,22 +121,23 @@ def tile_drug_restart_scores_s10_kernel(
         load_far_scales(1)
         load_far(3)
         load_far(4)
-        load_x(3)
-        load_x(4)
+        load_x(3,0,4)
+        load_x(4,0,4)
+        load_x_quadrants()
+        load_modules(0,0)
         load_walk_scales_packed()
-        load_modules(0, 0)
-        load_modules(1, 0)
+        load_walk(0,5,0)
         load_walk_scales_last()
-        load_walk(0, 5, 0)
-        load_modules(2, 0)
-        load_modules(3, 0)
-        load_modules(4, 0)
-        load_modules(0, 1)
-        load_modules(1, 1)
-        load_modules(2, 1)
-        load_walk(0, 5, 1)
-        load_modules(3, 1)
-        load_modules(4, 1)
+        load_modules(1,0)
+        load_modules(2,0)
+        load_modules(3,0)
+        load_modules(4,0)
+        load_modules(0,1)
+        load_modules(1,1)
+        load_walk(0,5,1)
+        load_modules(2,1)
+        load_modules(3,1)
+        load_modules(4,1)
 
 
         ordered = {}
@@ -190,32 +189,21 @@ def tile_drug_restart_scores_s10_kernel(
         v_sorted = {}
         v_turned = {}
 
-        def sort_quads(m, b, engine_copy):
-            if m not in v_sorted:
-                v_sorted[m] = stage.tile([P, 2, G * P], F32, name="x_ordered", align_bytes=256)
-            t = v_sorted[m][:].rearrange("p u w -> p (u w)").rearrange("p (g b e u w) -> p g b e u w", g=G, b=2, e=2, u=2)
-            words = x_quads[m, b][:].rearrange("p j c -> p (j c)").bitcast(F32)
-            engine_copy(
-                out=t[:, :, b, :, :, :].rearrange("p g e u w -> p e g u w"),
-                in_=words.rearrange("p (e g w u) -> p e g u w", e=2, g=G, u=2),
-            )
+        def sort_quads(engine_copy):
+            t = keep.tile([P, 2, 8, 32], F32, name="v_sorted", align_bytes=256)
+            words = x_quads[0][:].rearrange("p b c -> p (b c)").bitcast(F32)
+            engine_copy(out=t[:].rearrange("p u b w -> p u (b w)"), in_=words.rearrange("p (w u) -> p u w", u=2))
+            v_sorted[0] = t
 
-        def turn_quads(piece):
-            m, g0 = piece[0]
-            n = len(piece)
-            t = stage.tile([P, 512], F32, name="v_turned", align_bytes=256, bufs=3)
-            flat = v_sorted[m][:].rearrange("p u w -> p (u w)")
-            nc.vector.transpose(t[:, 0 : 256 * n], flat[:, 256 * g0 : 256 * (g0 + n)])
-            v_turned[piece] = t
+        def turn_quads():
+            t = keep.tile([P, 2, 256], F32, name="v_turned", align_bytes=256)
+            nc.vector.transpose(t[:].rearrange("p u c -> p (u c)"), v_sorted[0][:].rearrange("p u b w -> p (u b w)"))
+            v_turned[0] = t
 
         def pair_quads(piece, engine_copy):
-            n = len(piece)
             t = stage.tile([P, 2, P, 4], BF16, name="x_grouped", align_bytes=256, bufs=4)
-            words = t[:].rearrange("p c r j -> p (c r j)").bitcast(F32)[:, 0 : 256 * n]
-            engine_copy(
-                out=words.rearrange("p (c i r) -> p c i r", i=32, r=4),
-                in_=v_turned[piece][:, 0 : 256 * n].rearrange("p (c r i) -> p c i r", i=32, r=4),
-            )
+            words = t[:].rearrange("p c r j -> p (c r j)").bitcast(F32)
+            engine_copy(out=words.rearrange("p (c u) -> p c u", u=2), in_=v_turned[0][:].rearrange("p u c -> p c u"))
             grouped[piece] = t
 
         d_grouped = {}
@@ -359,75 +347,122 @@ def tile_drug_restart_scores_s10_kernel(
             transpose_x(piece, b)
         take(third)
         reorder_x(3, 0, 2, scopy)
-        reorder_x(3, 2, 5, vcopy)
+        reorder_x(3, 2, 4, vcopy)
         for m, g in ((0, 3), (1, 3), (0, 4), (1, 4)):
             far_passes(m, g)
-        reorder_x(4, 0, 5, vcopy)
+        reorder_x(4, 0, 2, vcopy)
+        reorder_x(4, 2, 4, vcopy)
         keep_far(0, 0)
         keep_far(0, 1)
         keep_far(1, 0)
-        keep_far(1, 1)
         rest = pieces(3, 4)
-        acc["far", 2, 0, 0] = psum.tile([P, NH], F32, name="bank4")
-        for g in range(3):
-            one_pass("far", 2, 0, g)
-        transpose_x(rest[0], 5)
-        transpose_x(rest[1], 6)
-        for g in range(3, G):
-            one_pass("far", 2, 0, g)
-        transpose_x(rest[4], 7)
-        transpose_x(rest[2], 0)
-        transpose_x(rest[3], 1)
-        take([rest[0], rest[1], rest[4], rest[2], rest[3]])
-        product("far", 2, 1, 2)
+        product("far", 2, 0, 4)
+        for piece, b in zip(rest[:4], (6, 7, 0, 1)):
+            transpose_x(piece, b)
+        product("far", 2, 1, 5)
+        keep_far(1, 1)
+        sort_quads(vcopy)
+        copy_x(rest[0], scopy)
+        turn_quads()
+        copy_x(rest[1], scopy)
+        quantize_x(rest[0])
+        pair_quads(rest[4], vcopy)
+        quantize_x(rest[1])
+        copy_x(rest[2], scopy)
+        quantize_x(rest[4])
+        copy_x(rest[3], vcopy)
         keep_far(2, 0)
-        copy_d(1, 0, scopy, 0, 256)
+        quantize_x(rest[2])
+        quantize_x(rest[3])
         product("far", 3, 0, 3)
-        copy_d(0, 0, vcopy)
-        copy_d(1, 0, scopy, 256, 512)
         keep_far(2, 1)
-
-        steps = [("far", 3, 1), ("far", 4, 0)]
-        steps = steps + [(kind, m, h) for h in range(H) for kind in ("walk", "direct") for m in range(MT)]
-        last = len(steps) - 1
-        walk0, direct0, walk1 = 2, 2 + MT, 2 + 2 * MT
-        vector_at = {walk0: (2, 0), walk0 + 2: (4, 0), walk1 + 1: (G - 1, 1)}
-        scalar_at = {walk0 + 1: (3, 0, 0), walk0 + 2: (3, 0, 256)}
-        for g in range(G - 1):
-            scalar_at[direct0 + 2 * g] = (g, 1, 0)
-            scalar_at[direct0 + 2 * g + 1] = (g, 1, 256)
-        quantize_at = {0: (0, 0), 1: (1, 0), walk0 + 3: (3, 0), walk1 - 1: (0, 1), walk1: (1, 1), walk1 + 2: (2, 1)}
-        quantize_at[walk0 + 1] = (2, 0)
-        quantize_at[walk0 + 4] = (4, 0)
-        quantize_at[walk1 + 3] = (G - 1, 1)
-        quantize_at[walk1 + 4] = (3, 1)
-        before = ("far", 3, 0)
-        for s, (kind, m, h) in enumerate(steps):
-            bank = (4 + s) % 8
-            if s == last:
-                break
-            product(kind, m, h, bank)
-            if before[0] == "far":
-                keep_far(*before[1:])
-            if before[0] == "walk":
-                restart(*before[1:])
-            if s in scalar_at:
-                g, hh, c = scalar_at[s]
-                copy_d(g, hh, scopy, c, c + 256)
-            if s in quantize_at:
-                quantize_d(*quantize_at[s])
-            if s in vector_at:
-                copy_d(*vector_at[s], vcopy)
-            if s >= 2 and steps[s - 2][0] == "walk" and steps[s - 2][1:] != (MT - 1, H - 1):
-                weigh_far(*steps[s - 2][1:])
-            if before[0] == "direct" and before[2] == 0:
-                weigh_direct(before[1], 0, 0, NH)
-            if s >= 2 and steps[s - 2][0] == "direct" and steps[s - 2][2] == 0:
-                add_up(steps[s - 2][1], 0, 0, NH)
-                store(steps[s - 2][1], 0, 0, NH)
-            if before[0] == "direct" and before[2] == 1:
-                finish(before[1], 1)
-            before = (kind, m, h)
+        product("far", 3, 1, 4)
+        keep_far(3, 0)
+        copy_d(0, 0, vcopy)
+        product("far", 4, 0, 5)
+        keep_far(3, 1)
+        quantize_d(0, 0)
+        product("walk", 0, 0, 6)
+        keep_far(4, 0)
+        copy_d(1, 0, vcopy)
+        product("walk", 1, 0, 7)
+        restart(0, 0)
+        copy_d(2, 0, scopy, 0, 256)
+        quantize_d(1, 0)
+        copy_d(2, 0, vcopy, 256, 512)
+        product("walk", 2, 0, 0)
+        restart(1, 0)
+        copy_d(3, 0, scopy, 0, 256)
+        weigh_far(0, 0)
+        copy_d(3, 0, vcopy, 256, 512)
+        quantize_d(2, 0)
+        product("walk", 3, 0, 1)
+        copy_d(4, 0, scopy, 0, 256)
+        copy_d(4, 0, vcopy, 256, 512)
+        quantize_d(3, 0)
+        weigh_far(1, 0)
+        quantize_d(4, 0)
+        restart(2, 0)
+        product("walk", 4, 0, 2)
+        restart(3, 0)
+        restart(4, 0)
+        copy_d(0, 1, scopy, 0, 256)
+        for m in range(2):
+            acc["direct", m, 0, 0] = psum.tile([P, NH], F32, name="bank%d" % (3 + m))
+        for g in range(G):
+            for m in range(2):
+                one_pass("direct", m, 0, g)
+        weigh_far(2, 0)
+        weigh_far(3, 0)
+        weigh_far(4, 0)
+        copy_d(0, 1, scopy, 256, 512)
+        copy_d(1, 1, scopy)
+        product("direct", 2, 0, 5)
+        weigh_direct(0, 0, 0, NH)
+        weigh_direct(1, 0, 0, NH)
+        add_up(0, 0, 0, NH)
+        store(0, 0, 0, NH)
+        product("direct", 3, 0, 6)
+        add_up(1, 0, 0, NH)
+        store(1, 0, 0, NH)
+        weigh_direct(2, 0, 0, NH)
+        quantize_d(0, 1)
+        add_up(2, 0, 0, NH)
+        store(2, 0, 0, NH)
+        product("direct", 4, 0, 7)
+        copy_d(2, 1, scopy)
+        weigh_direct(3, 0, 0, NH)
+        quantize_d(1, 1)
+        add_up(3, 0, 0, NH)
+        store(3, 0, 0, NH)
+        product("walk", 0, 1, 0)
+        weigh_direct(4, 0, 0, NH)
+        copy_d(3, 1, vcopy, 0, 256)
+        add_up(4, 0, 0, NH)
+        store(4, 0, 0, NH)
+        product("walk", 1, 1, 1)
+        restart(0, 1)
+        copy_d(3, 1, scopy, 256, 512)
+        quantize_d(2, 1)
+        product("walk", 2, 1, 2)
+        restart(1, 1)
+        copy_d(4, 1, vcopy)
+        quantize_d(3, 1)
+        product("walk", 3, 1, 3)
+        restart(2, 1)
+        quantize_d(4, 1)
+        weigh_far(0, 1)
+        weigh_far(1, 1)
+        product("walk", 4, 1, 4)
+        restart(3, 1)
+        weigh_far(2, 1)
+        product("direct", 0, 1, 5)
+        restart(4, 1)
+        weigh_far(3, 1)
+        for m in range(1, MT - 1):
+            product("direct", m, 1, (5 + m) % 8)
+            finish(m - 1, 1)
+        bank = 1
         m, h = MT - 1, H - 1
         r = r_sb[m, h]
         nc.scalar.activation(out=r[:], in_=r[:], func=COPY, scale=-0.5, bias=0.5)

@@ -361,29 +361,33 @@ def tile_drug_restart_scores_s10_kernel(
             transpose_x(piece, b)
         product("far", 2, 1, 5)
         keep_far(1, 1)
-        sort_quads(vcopy)
         copy_x(rest[0], scopy)
-        turn_quads()
         copy_x(rest[1], scopy)
-        quantize_x(rest[0])
-        pair_quads(rest[4], vcopy)
-        quantize_x(rest[1])
         copy_x(rest[2], scopy)
-        quantize_x(rest[4])
-        copy_x(rest[3], vcopy)
-        keep_far(2, 0)
+        copy_x(rest[3], scopy)
+        quantize_x(rest[0])
+        sort_quads(vcopy)
+        quantize_x(rest[1])
+        turn_quads()
         quantize_x(rest[2])
+        pair_quads(rest[4], vcopy)
         quantize_x(rest[3])
-        product("far", 3, 0, 3)
+        quantize_x(rest[4])
+        keep_far(2, 0)
         keep_far(2, 1)
-        product("far", 3, 1, 4)
-        keep_far(3, 0)
+        late = ((3, 0, 3), (3, 1, 2), (4, 0, 4))
+        for m, h, b in late:
+            acc["far", m, h, 0] = psum.tile([P, NH], F32, name="bank%d" % b)
+            for g in range(G - 1):
+                one_pass("far", m, h, g)
+        for m, h, b in late:
+            one_pass("far", m, h, G - 1)
         copy_d(0, 0, vcopy)
-        product("far", 4, 0, 5)
-        keep_far(3, 1)
-        quantize_d(0, 0)
         product("walk", 0, 0, 6)
+        keep_far(3, 0)
+        keep_far(3, 1)
         keep_far(4, 0)
+        quantize_d(0, 0)
         copy_d(1, 0, vcopy)
         product("walk", 1, 0, 7)
         restart(0, 0)

@@ -18,10 +18,18 @@ TANH = mybir.ActivationFunctionType.Tanh
 COPY = mybir.ActivationFunctionType.Copy
 
 P = 128
-G = K // 512
+QUAD = 32
+GENES = 512
+PAIRS = GENES // 2
+G = K // GENES
+LAST_G = G - 1
 MT = D // P
 NH = 512
 H = N // NH
+BANKS = 8
+FAR_SPLIT = 3
+SHARE = NH // 2
+TAIL = 128
 
 
 def tile_drug_restart_scores_s10_kernel(
@@ -33,467 +41,473 @@ def tile_drug_restart_scores_s10_kernel(
         stage = ctx.enter_context(tc.tile_pool(name="stage", bufs=2))
         psum = ctx.enter_context(tc.psum_pool(name="psum", bufs=1))
         ctx.enter_context(tc.manual_schedule())
-        vcopy = nc.vector.tensor_copy
-        scopy = nc.scalar.copy
+        on_vector = nc.vector.tensor_copy
+        on_scalar = nc.scalar.copy
 
-        ident = keep.tile([P, P], F32, name="ident", align_bytes=256)
-        f_words = [keep.tile([P, 2 * N], U8, name="f_words%d" % g, align_bytes=256) for g in range(G)]
-        f_runs = [(0, 3), (3, G)]
-        f_scales = [keep.tile([P, g1 - g0, N], U8, name="f_scales%d" % g0, align_bytes=256) for g0, g1 in f_runs]
-        w_words = {}
-        w_scales = [keep.tile([P, N], U8, name="w_scales%d" % i, align_bytes=256) for i in range(2)]
-        d_raw = [[keep.tile([P, 4, NH], BF16, name="d_raw%d%d" % (g, h), align_bytes=256) for h in range(H)] for g in range(G)]
-        d_codes = keep.tile([P, G, N], U32, name="d_codes", align_bytes=256)
-        d_scales = keep.tile([P, G, N], U8, name="d_scales", align_bytes=256)
-        pairs = [(m, h) for h in range(H) for m in range(MT)]
-        f_sb = {mh: keep.tile([P, NH], F32, name="f_sb%d%d" % mh, align_bytes=256) for mh in pairs}
-        r_sb = {mh: keep.tile([P, NH], F32, name="r_sb%d%d" % mh, align_bytes=256) for mh in pairs}
+        def kept(shape, dtype, name):
+            return keep.tile(shape, dtype, name=name, align_bytes=256)
 
-        x_raw = {}
-        x_quads = {}
+        def bank_tile(shape, bank):
+            return psum.tile(shape, F32, name="bank%d" % bank)
 
-        def load_x(m, g0=0, g1=G):
-            t = keep.tile([P, 512 * (g1 - g0)], BF16, name="x_raw%d%d" % (m, g0), align_bytes=256)
-            nc.sync.dma_start(out=t[:], in_=seeds[m * P : (m + 1) * P, 512 * g0 : 512 * g1])
+        ident = kept([P, P], F32, "ident")
+        far_w = [kept([P, 2 * N], U8, "far_w%d" % g) for g in range(G)]
+        far_runs = [(0, FAR_SPLIT), (FAR_SPLIT, G)]
+        far_s = [kept([P, g1 - g0, N], U8, "far_s%d" % g0) for g0, g1 in far_runs]
+        walk_w = {}
+        walk_s = [kept([P, N], U8, "walk_s%d" % i) for i in range(2)]
+        mod_raw = [[kept([P, 4, NH], BF16, "mod_raw%d%d" % (g, h)) for h in range(H)] for g in range(G)]
+        mod_codes = kept([P, G, N], U32, "mod_codes")
+        mod_scales = kept([P, G, N], U8, "mod_scales")
+        results = [(m, h) for h in range(H) for m in range(MT)]
+        far_sb = {mh: kept([P, NH], F32, "far_sb%d%d" % mh) for mh in results}
+        res_sb = {mh: kept([P, NH], F32, "res_sb%d%d" % mh) for mh in results}
+
+        seeds_raw = {}
+
+        def load_seeds(m, g0, g1):
+            t = kept([P, GENES * (g1 - g0)], BF16, "seeds_raw%d%d" % (m, g0))
+            nc.sync.dma_start(out=t[:], in_=seeds[m * P : (m + 1) * P, GENES * g0 : GENES * g1])
             for g in range(g0, g1):
-                x_raw[m, g] = (t, g0)
+                seeds_raw[m, g] = (t, g0)
 
-        def load_x_quadrants():
-            t = keep.tile([P, 8, P], BF16, name="x_raw00", align_bytes=256)
-            rows = seeds[3 * P : 5 * P, 512 * (G - 1) :].rearrange("(b i) (a c) -> i b a c", i=32, c=P)
+        def load_seeds_by_quadrant():
+            t = kept([P, 2 * P // QUAD, P], BF16, "seeds_raw00")
+            rows = seeds[3 * P : 5 * P, GENES * LAST_G :].rearrange("(b i) (a c) -> i b a c", i=QUAD, c=P)
             for a in (0, 2, 1, 3):
-                nc.sync.dma_start(out=t[32 * a : 32 * (a + 1), :, :], in_=rows[:, :, a, :])
-            x_quads[0] = t
+                nc.sync.dma_start(out=t[QUAD * a : QUAD * (a + 1), :, :], in_=rows[:, :, a, :])
+            return t
 
         def load_far(g):
-            nc.sync.dma_start(out=f_words[g][:].bitcast(I32), in_=far_words.bitcast(I32)[g])
+            nc.sync.dma_start(out=far_w[g][:].bitcast(I32), in_=far_words.bitcast(I32)[g])
 
-        def load_walk(g0, g1, h):
-            t = keep.tile([P, g1 - g0, NH], U32, name="w_words%d%d" % (g0, h), align_bytes=256)
-            words = walk_words.rearrange("g p n t -> g p (n t)").bitcast(I32)
-            nc.sync.dma_start(
-                out=t[:].bitcast(I32), in_=words[g0:g1, :, h * NH : (h + 1) * NH].rearrange("g p w -> p g w")
-            )
-            for g in range(g0, g1):
-                w_words[g, h] = t[:, g - g0, :]
-
-        def load_far_scales(i):
-            g0, g1 = f_runs[i]
+        def load_far_scales(run):
+            g0, g1 = far_runs[run]
             for r in range(4):
                 nc.sync.dma_start(
-                    out=f_scales[i][:].bitcast(I32)[r:P:32, :, :],
+                    out=far_s[run][:].bitcast(I32)[r:P:QUAD, :, :],
                     in_=far_scales.bitcast(I32)[g0:g1, r:16:4, :].rearrange("g q w -> q g w"),
                 )
+
+        def load_walk(h):
+            walk_w[h] = kept([P, G, NH], U32, "walk_w%d" % h)
+            words = walk_words.rearrange("g p n t -> g p (n t)").bitcast(I32)
+            nc.sync.dma_start(
+                out=walk_w[h][:].bitcast(I32), in_=words[:, :, h * NH : (h + 1) * NH].rearrange("g p w -> p g w")
+            )
 
         def load_walk_scales_packed():
             for q in range(4):
                 nc.sync.dma_start(
-                    out=w_scales[0][:].bitcast(I32)[32 * q : 32 * q + 16, :],
-                    in_=walk_scales.bitcast(I32)[0:4, 4 * q : 4 * q + 4, :],
+                    out=walk_s[0][:].bitcast(I32)[QUAD * q : QUAD * q + 16, :],
+                    in_=walk_scales.bitcast(I32)[0:LAST_G, 4 * q : 4 * q + 4, :],
                 )
 
         def load_walk_scales_last():
             for r in range(4):
                 nc.sync.dma_start(
-                    out=w_scales[1][:].bitcast(I32)[r:P:32, :], in_=walk_scales.bitcast(I32)[4, r:16:4, :]
+                    out=walk_s[1][:].bitcast(I32)[r:P:QUAD, :], in_=walk_scales.bitcast(I32)[LAST_G, r:16:4, :]
                 )
 
         def load_modules(g, h):
-            rows = modules[512 * g : 512 * (g + 1), h * NH : (h + 1) * NH]
-            nc.sync.dma_start(out=d_raw[g][h][:], in_=rows.rearrange("(p j) w -> p j w", j=4))
+            rows = modules[GENES * g : GENES * (g + 1), h * NH : (h + 1) * NH]
+            nc.sync.dma_start(out=mod_raw[g][h][:], in_=rows.rearrange("(p j) w -> p j w", j=4))
 
         make_identity(nc, ident[:])
-        nc.vector.memset(f_scales[0][:].bitcast(I32), 0)
-        nc.vector.memset(f_scales[1][:].bitcast(I32), 0)
-        nc.vector.memset(w_scales[0][:].bitcast(I32), 0)
-        nc.vector.memset(w_scales[1][:].bitcast(I32), 0)
-        nc.vector.memset(d_codes[:, G - 1, 0:NH], 0)
-        nc.vector.memset(d_scales[:, G - 1, 0:NH].bitcast(I32), 0)
+        nc.vector.memset(far_s[0][:].bitcast(I32), 0)
+        nc.vector.memset(far_s[1][:].bitcast(I32), 0)
+        nc.vector.memset(walk_s[0][:].bitcast(I32), 0)
+        nc.vector.memset(walk_s[1][:].bitcast(I32), 0)
+        nc.vector.memset(mod_codes[:, LAST_G, 0:NH], 0)
+        nc.vector.memset(mod_scales[:, LAST_G, 0:NH].bitcast(I32), 0)
 
-        load_x(0,0,2)
-        load_x(0,2,5)
-        load_x(1)
+        load_seeds(0, 0, 2)
+        load_seeds(0, 2, G)
+        load_seeds(1, 0, G)
         load_far_scales(0)
-        load_far(0)
-        load_far(1)
-        load_far(2)
-        load_x(2)
+        for g in range(FAR_SPLIT):
+            load_far(g)
+        load_seeds(2, 0, G)
         load_far_scales(1)
-        load_far(3)
-        load_far(4)
-        load_x(3,0,4)
-        load_x(4,0,4)
-        load_x_quadrants()
-        load_modules(0,0)
+        for g in range(FAR_SPLIT, G):
+            load_far(g)
+        load_seeds(3, 0, LAST_G)
+        load_seeds(4, 0, LAST_G)
+        quadrant_raw = load_seeds_by_quadrant()
+        load_modules(0, 0)
         load_walk_scales_packed()
-        load_walk(0,5,0)
+        load_walk(0)
         load_walk_scales_last()
-        load_modules(1,0)
-        load_modules(2,0)
-        load_modules(3,0)
-        load_modules(4,0)
-        load_modules(0,1)
-        load_modules(1,1)
-        load_walk(0,5,1)
-        load_modules(2,1)
-        load_modules(3,1)
-        load_modules(4,1)
+        for g in range(1, G):
+            load_modules(g, 0)
+        for g in range(2):
+            load_modules(g, 1)
+        load_walk(1)
+        for g in range(2, G):
+            load_modules(g, 1)
 
-
-        ordered = {}
-        sorted_words = {}
+        sorted_tiles = {}
+        sorted_chunks = {}
         turned = {}
         grouped = {}
-        x_operands = {}
+        stationary = {}
 
-        def reorder_x(m, g0, g1, engine_copy):
-            if m not in sorted_words:
-                sorted_words[m] = stage.tile([P, 2, G * P], F32, name="x_ordered", align_bytes=256)
-            t = sorted_words[m]
-            raw, base = x_raw[m, g0]
-            words = raw[:].bitcast(F32)[:, 256 * (g0 - base) : 256 * (g1 - base)]
-            engine_copy(out=t[:, :, P * g0 : P * g1], in_=words.rearrange("r (w u) -> r u w", u=2))
+        def raw_pairs(m, g0, g1):
+            t, base = seeds_raw[m, g0]
+            return t[:].bitcast(F32)[:, PAIRS * (g0 - base) : PAIRS * (g1 - base)]
+
+        def sort_pairs(m, g0, g1, copy):
+            if m not in sorted_tiles:
+                sorted_tiles[m] = stage.tile([P, 2, G * P], F32, name="seeds_sorted", align_bytes=256)
+            t = sorted_tiles[m]
+            copy(out=t[:, :, P * g0 : P * g1], in_=raw_pairs(m, g0, g1).rearrange("r (w u) -> r u w", u=2))
             for g in range(g0, g1):
-                ordered[m, g] = t[:, :, P * g : P * (g + 1)]
+                sorted_chunks[m, g] = t[:, :, P * g : P * (g + 1)]
 
-        def transpose_x(piece, b):
-            bank = psum.tile([P, 2, 2, P], F32, name="bank%d" % b)
+        def transpose(piece, bank):
+            turned[piece] = bank_tile([P, 2, 2, P], bank)
             for j, (m, g) in enumerate(piece):
                 for u in range(2):
-                    if (m, g) in ordered:
-                        src = ordered[m, g][:, u, :]
+                    if (m, g) in sorted_chunks:
+                        src = sorted_chunks[m, g][:, u, :]
                     else:
-                        raw, base = x_raw[m, g]
-                        src = raw[:].bitcast(F32)[:, 256 * (g - base) + u : 256 * (g - base + 1) : 2]
-                    nc.tensor.transpose(bank[:, j, u, :], src, ident[:])
-            turned[piece] = bank
+                        src = raw_pairs(m, g, g + 1)[:, u:PAIRS:2]
+                    nc.tensor.transpose(turned[piece][:, j, u, :], src, ident[:])
 
-        def copy_x(piece, engine_copy):
-            n = len(piece)
-            t = stage.tile([P, 2, P, 4], BF16, name="x_grouped", align_bytes=256, bufs=4)
-            engine_copy(out=t[:].bitcast(F32)[:, 0:n], in_=turned[piece][:, 0:n, :, :].rearrange("p c u r -> p c r u"))
-            grouped[piece] = t
+        def grouped_tile(piece):
+            grouped[piece] = stage.tile([P, 2, P, 4], BF16, name="seeds_grouped", align_bytes=256, bufs=4)
+            return grouped[piece]
 
-        def quantize_x(piece):
+        def group(piece, copy):
             n = len(piece)
-            codes = keep.tile([P, n * P], U32, name="x_codes%d%d" % piece[0], align_bytes=256)
-            scales = keep.tile([P, n * P], U8, name="x_scales%d%d" % piece[0], align_bytes=256)
+            t = grouped_tile(piece)
+            copy(out=t[:].bitcast(F32)[:, 0:n], in_=turned[piece][:, 0:n, :, :].rearrange("p c u r -> p c r u"))
+
+        def quantize_seeds(piece):
+            n = len(piece)
+            codes = kept([P, n * P], U32, "seeds_codes%d%d" % piece[0])
+            scales = kept([P, n * P], U8, "seeds_scales%d%d" % piece[0])
             nc.vector.quantize_mx(
                 out=codes[:].bitcast(E4M3),
                 scales=scales[:],
                 in_=grouped[piece][:, 0:n].rearrange("p c r j -> p (c r j)"),
             )
             for j, chunk in enumerate(piece):
-                x_operands[chunk] = (codes[:, j * P : (j + 1) * P], scales[:, j * P : (j + 1) * P])
+                stationary[chunk] = (codes[:, j * P : (j + 1) * P], scales[:, j * P : (j + 1) * P])
 
-        v_sorted = {}
-        v_turned = {}
+        def pieces(m):
+            return [((m, 0), (m, 1)), ((m, 2), (m, 3)), ((m, 4),)]
 
-        def sort_quads(engine_copy):
-            t = keep.tile([P, 2, 8, 32], F32, name="v_sorted", align_bytes=256)
-            words = x_quads[0][:].rearrange("p b c -> p (b c)").bitcast(F32)
-            engine_copy(out=t[:].rearrange("p u b w -> p u (b w)"), in_=words.rearrange("p (w u) -> p u w", u=2))
-            v_sorted[0] = t
+        quadrant_sorted = kept([P, 2, 2 * P], F32, "quadrant_sorted")
+        quadrant_turned = kept([P, 2, 2 * P], F32, "quadrant_turned")
 
-        def turn_quads():
-            t = keep.tile([P, 2, 256], F32, name="v_turned", align_bytes=256)
-            nc.vector.transpose(t[:].rearrange("p u c -> p (u c)"), v_sorted[0][:].rearrange("p u b w -> p (u b w)"))
-            v_turned[0] = t
+        def sort_quadrants():
+            words = quadrant_raw[:].rearrange("p b c -> p (b c)").bitcast(F32)
+            on_vector(out=quadrant_sorted[:], in_=words.rearrange("p (w u) -> p u w", u=2))
 
-        def pair_quads(piece, engine_copy):
-            t = stage.tile([P, 2, P, 4], BF16, name="x_grouped", align_bytes=256, bufs=4)
-            words = t[:].rearrange("p c r j -> p (c r j)").bitcast(F32)
-            engine_copy(out=words.rearrange("p (c u) -> p c u", u=2), in_=v_turned[0][:].rearrange("p u c -> p c u"))
-            grouped[piece] = t
-
-        d_grouped = {}
-
-        def copy_d(g, h, engine_copy, c0=0, c1=NH):
-            if c0 == 0:
-                d_grouped[g, h] = stage.tile([P, NH, 4], BF16, name="d_grouped", align_bytes=256, bufs=4)
-            engine_copy(
-                out=d_grouped[g, h][:, c0:c1, :].rearrange("p (c i) j -> p c j i", i=4),
-                in_=d_raw[g][h][:, :, c0:c1].rearrange("p j (c i) -> p c j i", i=4),
+        def transpose_quadrants():
+            nc.vector.transpose(
+                quadrant_turned[:].rearrange("p u c -> p (u c)"), quadrant_sorted[:].rearrange("p u w -> p (u w)")
             )
 
-        def quantize_d(g, h):
+        def group_quadrants(piece):
+            words = grouped_tile(piece)[:].rearrange("p c r j -> p (c r j)").bitcast(F32)
+            on_vector(out=words.rearrange("p (c u) -> p c u", u=2), in_=quadrant_turned[:].rearrange("p u c -> p c u"))
+
+        mod_grouped = {}
+
+        def interleave(g, h, copy, c0=0, c1=NH):
+            if c0 == 0:
+                mod_grouped[g, h] = stage.tile([P, NH, 4], BF16, name="mod_grouped", align_bytes=256, bufs=4)
+            copy(
+                out=mod_grouped[g, h][:, c0:c1, :].rearrange("p (c i) j -> p c j i", i=4),
+                in_=mod_raw[g][h][:, :, c0:c1].rearrange("p j (c i) -> p c j i", i=4),
+            )
+
+        def quantize_modules(g, h):
             cols = slice(h * NH, (h + 1) * NH)
             nc.vector.quantize_mx(
-                out=d_codes[:, g, cols].bitcast(E4M3),
-                scales=d_scales[:, g, cols],
-                in_=d_grouped[g, h][:].rearrange("p w j -> p (w j)"),
+                out=mod_codes[:, g, cols].bitcast(E4M3),
+                scales=mod_scales[:, g, cols],
+                in_=mod_grouped[g, h][:].rearrange("p w j -> p (w j)"),
             )
 
-        acc = {}
+        sums = {}
+
+        def open_sum(kind, m, h, bank, c0=0):
+            sums[kind, m, h, c0] = bank_tile([P, NH], bank % BANKS)
 
         def one_pass(kind, m, h, g, c0=0, c1=NH):
             n0, n1 = h * NH + c0, h * NH + c1
             if kind == "far":
-                rhs, scale = f_words[g][:, 2 * n0 : 2 * n1].bitcast(E2M1), f_scales[g // 3][:, g % 3, n0:n1]
+                rhs = far_w[g][:, 2 * n0 : 2 * n1].bitcast(E2M1)
+                rhs_scale = far_s[g // FAR_SPLIT][:, g % FAR_SPLIT, n0:n1]
             elif kind == "walk":
-                rhs = w_words[g, h][:, c0:c1].bitcast(E4M3)
-                scale = w_scales[g // 4][4 * (g % 4) :, n0:n1]
+                rhs = walk_w[h][:, g, c0:c1].bitcast(E4M3)
+                rhs_scale = walk_s[g // LAST_G][4 * (g % LAST_G) :, n0:n1]
             else:
-                rhs, scale = d_codes[:, g, n0:n1].bitcast(E4M3), d_scales[:, g, n0:n1]
-            codes, scales = x_operands[m, g]
+                rhs = mod_codes[:, g, n0:n1].bitcast(E4M3)
+                rhs_scale = mod_scales[:, g, n0:n1]
+            codes, scales = stationary[m, g]
             nc.tensor.matmul_mx(
-                out=acc[kind, m, h, c0][:, c0:c1],
+                out=sums[kind, m, h, c0][:, c0:c1],
                 lhsT=codes.bitcast(E4M3),
                 lhsT_scale=scales,
                 rhs=rhs,
-                rhs_scale=scale,
+                rhs_scale=rhs_scale,
                 start=(g == 0),
-                stop=(g == G - 1),
+                stop=(g == LAST_G),
             )
 
         def product(kind, m, h, bank, c0=0, c1=NH):
-            acc[kind, m, h, c0] = psum.tile([P, NH], F32, name="bank%d" % bank)
+            open_sum(kind, m, h, bank, c0)
             for g in range(G):
                 one_pass(kind, m, h, g, c0, c1)
-
-        def keep_far(m, h):
-            nc.scalar.activation(out=f_sb[m, h][:], in_=acc["far", m, h, 0][:], func=COPY, scale=0.5)
-
-        def restart(m, h):
-            nc.scalar.activation(out=r_sb[m, h][:], in_=acc["walk", m, h, 0][:], func=TANH, scale=0.5)
-
-        def weigh_far(m, h):
-            nc.vector.scalar_tensor_tensor(
-                out=f_sb[m, h][:], in0=r_sb[m, h][:], scalar=1.0, in1=f_sb[m, h][:], op0=ALU.add, op1=ALU.mult
-            )
-
-        def weigh_direct(m, h, c0, c1, group=0):
-            r = r_sb[m, h][:, c0:c1]
-            nc.vector.scalar_tensor_tensor(
-                out=r, in0=r, scalar=1.0, in1=acc["direct", m, h, group][:, c0:c1], op0=ALU.subtract, op1=ALU.mult
-            )
-
-        def add_up(m, h, c0, c1):
-            r = r_sb[m, h][:, c0:c1]
-            nc.vector.scalar_tensor_tensor(
-                out=r, in0=r, scalar=-0.5, in1=f_sb[m, h][:, c0:c1], op0=ALU.mult, op1=ALU.add
-            )
-
-        def store(m, h, c0, c1):
-            nc.sync.dma_start(out=out[m * P : (m + 1) * P, h * NH + c0 : h * NH + c1], in_=r_sb[m, h][:, c0:c1])
-
-        def finish(m, h):
-            weigh_direct(m, h, 0, 256)
-            weigh_direct(m, h, 256, 512)
-            add_up(m, h, 0, 256)
-            add_up(m, h, 256, 512)
-            store(m, h, 0, 512)
 
         def far_passes(m, g):
             for h in range(H):
                 one_pass("far", m, h, g)
 
-        def warm_up(count, b):
-            bank = psum.tile([P, NH], F32, name="bank%d" % b)
+        def warm_up(count):
+            bank = bank_tile([P, NH], 3)
             for i in range(count):
                 nc.tensor.matmul_mx(
                     out=bank[:],
-                    lhsT=d_codes[:, G - 1, 0:P].bitcast(E4M3),
-                    lhsT_scale=d_scales[:, G - 1, 0:P],
-                    rhs=d_codes[:, G - 1, 0:NH].bitcast(E4M3),
-                    rhs_scale=d_scales[:, G - 1, 0:NH],
+                    lhsT=mod_codes[:, LAST_G, 0:P].bitcast(E4M3),
+                    lhsT_scale=mod_scales[:, LAST_G, 0:P],
+                    rhs=mod_codes[:, LAST_G, 0:NH].bitcast(E4M3),
+                    rhs_scale=mod_scales[:, LAST_G, 0:NH],
                     start=True,
                     stop=True,
                 )
 
-        def pieces(ma, mb):
-            return [((ma, 0), (ma, 1)), ((ma, 2), (ma, 3)), ((mb, 0), (mb, 1)), ((mb, 2), (mb, 3)), ((ma, 4), (mb, 4))]
+        def keep_far(m, h):
+            nc.scalar.activation(out=far_sb[m, h][:], in_=sums["far", m, h, 0][:], func=COPY, scale=0.5)
 
-        def take(group):
-            for i, piece in enumerate(group):
-                copy_x(piece, (vcopy, scopy)[i % 2])
-                if i >= 1:
-                    quantize_x(group[i - 1])
-            quantize_x(group[-1])
+        def keep_tanh(m, h):
+            nc.scalar.activation(out=res_sb[m, h][:], in_=sums["walk", m, h, 0][:], func=TANH, scale=0.5)
 
-        first = pieces(0, 1)
-        warm_up(3, 3)
-        transpose_x(first[0], 4)
-        warm_up(2, 3)
-        reorder_x(0, 2, 5, vcopy)
-        transpose_x(first[1], 5)
-        warm_up(2, 3)
-        copy_x(first[0], scopy)
-        reorder_x(1, 0, 2, vcopy)
-        reorder_x(1, 4, 5, scopy)
-        reorder_x(1, 2, 4, vcopy)
-        transpose_x(first[2], 6)
-        transpose_x(first[3], 7)
-        transpose_x(first[4], 4)
-        copy_x(first[1], scopy)
-        quantize_x(first[0])
-        copy_x(first[2], vcopy)
-        copy_x(first[3], scopy)
-        quantize_x(first[1])
-        quantize_x(first[2])
-        copy_x(first[4], scopy)
-        quantize_x(first[3])
-        quantize_x(first[4])
+        def weigh_far(m, h):
+            nc.vector.scalar_tensor_tensor(
+                out=far_sb[m, h][:], in0=res_sb[m, h][:], scalar=1.0, in1=far_sb[m, h][:], op0=ALU.add, op1=ALU.mult
+            )
+
+        def weigh_direct(m, h, c0=0, c1=NH):
+            r = res_sb[m, h][:, c0:c1]
+            nc.vector.scalar_tensor_tensor(
+                out=r, in0=r, scalar=1.0, in1=sums["direct", m, h, 0][:, c0:c1], op0=ALU.subtract, op1=ALU.mult
+            )
+
+        def add_up(m, h, c0=0, c1=NH):
+            r = res_sb[m, h][:, c0:c1]
+            nc.vector.scalar_tensor_tensor(
+                out=r, in0=r, scalar=-0.5, in1=far_sb[m, h][:, c0:c1], op0=ALU.mult, op1=ALU.add
+            )
+
+        def store(m, h, c0=0, c1=NH):
+            nc.sync.dma_start(out=out[m * P : (m + 1) * P, h * NH + c0 : h * NH + c1], in_=res_sb[m, h][:, c0:c1])
+
+        def add_and_store(m, h):
+            add_up(m, h)
+            store(m, h)
+
+        def finish(m, h):
+            for c0 in (0, NH // 2):
+                weigh_direct(m, h, c0, c0 + NH // 2)
+            for c0 in (0, NH // 2):
+                add_up(m, h, c0, c0 + NH // 2)
+            store(m, h)
+
+        head0, mid0 = pieces(0)[:2]
+        head1, mid1 = pieces(1)[:2]
+        ends = ((0, LAST_G), (1, LAST_G))
+        warm_up(2)
+        transpose(head0, 4)
+        warm_up(2)
+        sort_pairs(0, 2, G, on_vector)
+        transpose(mid0, 5)
+        warm_up(2)
+        group(head0, on_scalar)
+        sort_pairs(1, 0, 2, on_vector)
+        sort_pairs(1, LAST_G, G, on_scalar)
+        sort_pairs(1, 2, LAST_G, on_vector)
+        transpose(head1, 6)
+        transpose(mid1, 7)
+        transpose(ends, 4)
+        group(mid0, on_scalar)
+        quantize_seeds(head0)
+        group(head1, on_vector)
+        group(mid1, on_scalar)
+        quantize_seeds(mid0)
+        quantize_seeds(head1)
+        group(ends, on_scalar)
+        quantize_seeds(mid1)
+        quantize_seeds(ends)
+
         for m in range(2):
             for h in range(H):
-                acc["far", m, h, 0] = psum.tile([P, NH], F32, name="bank%d" % (2 * m + h))
-        reorder_x(2, 0, 2, vcopy)
-        reorder_x(2, 4, 5, scopy)
-        reorder_x(2, 2, 4, vcopy)
-        for m, g in ((0, 0), (0, 1), (0, 2), (1, 0), (1, 1), (1, 2)):
-            far_passes(m, g)
-        third = [((2, 0), (2, 1)), ((2, 2), (2, 3)), ((2, 4),)]
-        for piece, b in zip(third, (5, 6, 7)):
-            transpose_x(piece, b)
-        take(third)
-        reorder_x(3, 0, 2, scopy)
-        reorder_x(3, 2, 4, vcopy)
-        for m, g in ((0, 3), (1, 3), (0, 4), (1, 4)):
-            far_passes(m, g)
-        reorder_x(4, 0, 2, vcopy)
-        reorder_x(4, 2, 4, vcopy)
+                open_sum("far", m, h, H * m + h)
+        sort_pairs(2, 0, 2, on_vector)
+        sort_pairs(2, LAST_G, G, on_scalar)
+        sort_pairs(2, 2, LAST_G, on_vector)
+        for m in range(2):
+            for g in range(FAR_SPLIT):
+                far_passes(m, g)
+        head2, mid2, end2 = pieces(2)
+        for bank, piece in enumerate((head2, mid2, end2), 5):
+            transpose(piece, bank)
+        group(head2, on_vector)
+        group(mid2, on_scalar)
+        quantize_seeds(head2)
+        group(end2, on_vector)
+        quantize_seeds(mid2)
+        quantize_seeds(end2)
+        sort_pairs(3, 0, 2, on_scalar)
+        sort_pairs(3, 2, LAST_G, on_vector)
+        for g in range(FAR_SPLIT, G):
+            for m in range(2):
+                far_passes(m, g)
+        sort_pairs(4, 0, 2, on_vector)
+        sort_pairs(4, 2, LAST_G, on_vector)
         keep_far(0, 0)
         keep_far(0, 1)
         keep_far(1, 0)
-        rest = pieces(3, 4)
+
+        head3, mid3 = pieces(3)[:2]
+        head4, mid4 = pieces(4)[:2]
+        by_quadrant = ((3, LAST_G), (4, LAST_G))
         product("far", 2, 0, 4)
-        for piece, b in zip(rest[:4], (6, 7, 0, 1)):
-            transpose_x(piece, b)
+        for piece, bank in zip((head3, mid3, head4, mid4), (6, 7, 0, 1)):
+            transpose(piece, bank)
         product("far", 2, 1, 5)
         keep_far(1, 1)
-        copy_x(rest[0], scopy)
-        copy_x(rest[1], scopy)
-        copy_x(rest[2], scopy)
-        copy_x(rest[3], scopy)
-        quantize_x(rest[0])
-        sort_quads(vcopy)
-        quantize_x(rest[1])
-        turn_quads()
-        quantize_x(rest[2])
-        pair_quads(rest[4], vcopy)
-        quantize_x(rest[3])
-        quantize_x(rest[4])
+        for piece in (head3, mid3, head4, mid4):
+            group(piece, on_scalar)
+        quantize_seeds(head3)
+        sort_quadrants()
+        quantize_seeds(mid3)
+        transpose_quadrants()
+        quantize_seeds(head4)
+        group_quadrants(by_quadrant)
+        quantize_seeds(mid4)
+        quantize_seeds(by_quadrant)
         keep_far(2, 0)
         keep_far(2, 1)
         late = ((3, 0, 3), (3, 1, 2), (4, 0, 4))
-        for m, h, b in late:
-            acc["far", m, h, 0] = psum.tile([P, NH], F32, name="bank%d" % b)
-            for g in range(G - 1):
+        for m, h, bank in late:
+            open_sum("far", m, h, bank)
+            for g in range(LAST_G):
                 one_pass("far", m, h, g)
-        for m, h, b in late:
-            one_pass("far", m, h, G - 1)
-        copy_d(0, 0, vcopy)
+        for m, h, bank in late:
+            one_pass("far", m, h, LAST_G)
+
+        interleave(0, 0, on_vector)
         product("walk", 0, 0, 6)
-        keep_far(3, 0)
-        keep_far(3, 1)
-        keep_far(4, 0)
-        quantize_d(0, 0)
-        copy_d(1, 0, vcopy)
+        for m, h, bank in late:
+            keep_far(m, h)
+        quantize_modules(0, 0)
+        interleave(1, 0, on_vector)
         product("walk", 1, 0, 7)
-        restart(0, 0)
-        copy_d(2, 0, scopy, 0, 256)
-        quantize_d(1, 0)
-        copy_d(2, 0, vcopy, 256, 512)
+        keep_tanh(0, 0)
+        interleave(2, 0, on_scalar, 0, SHARE)
+        quantize_modules(1, 0)
+        interleave(2, 0, on_vector, SHARE, NH)
         product("walk", 2, 0, 0)
-        restart(1, 0)
-        copy_d(3, 0, scopy, 0, 256)
+        keep_tanh(1, 0)
+        interleave(3, 0, on_scalar, 0, SHARE)
         weigh_far(0, 0)
-        copy_d(3, 0, vcopy, 256, 512)
-        quantize_d(2, 0)
+        interleave(3, 0, on_vector, SHARE, NH)
+        quantize_modules(2, 0)
         product("walk", 3, 0, 1)
-        copy_d(4, 0, scopy, 0, 256)
-        copy_d(4, 0, vcopy, 256, 512)
-        quantize_d(3, 0)
+        interleave(4, 0, on_scalar, 0, SHARE)
+        interleave(4, 0, on_vector, SHARE, NH)
+        quantize_modules(3, 0)
         weigh_far(1, 0)
-        quantize_d(4, 0)
-        restart(2, 0)
+        quantize_modules(4, 0)
+        keep_tanh(2, 0)
         product("walk", 4, 0, 2)
-        restart(3, 0)
-        restart(4, 0)
-        copy_d(0, 1, scopy, 0, 256)
+        keep_tanh(3, 0)
+        keep_tanh(4, 0)
+
+        interleave(0, 1, on_scalar, 0, SHARE)
         for m in range(2):
-            acc["direct", m, 0, 0] = psum.tile([P, NH], F32, name="bank%d" % (3 + m))
+            open_sum("direct", m, 0, 3 + m)
         for g in range(G):
             for m in range(2):
                 one_pass("direct", m, 0, g)
-        weigh_far(2, 0)
-        weigh_far(3, 0)
-        weigh_far(4, 0)
-        copy_d(0, 1, scopy, 256, 512)
-        copy_d(1, 1, scopy)
+        for m in range(2, MT):
+            weigh_far(m, 0)
+        interleave(0, 1, on_scalar, SHARE, NH)
+        interleave(1, 1, on_scalar)
         product("direct", 2, 0, 5)
-        weigh_direct(0, 0, 0, NH)
-        weigh_direct(1, 0, 0, NH)
-        add_up(0, 0, 0, NH)
-        store(0, 0, 0, NH)
+        weigh_direct(0, 0)
+        weigh_direct(1, 0)
+        add_and_store(0, 0)
         product("direct", 3, 0, 6)
-        add_up(1, 0, 0, NH)
-        store(1, 0, 0, NH)
-        weigh_direct(2, 0, 0, NH)
-        quantize_d(0, 1)
-        add_up(2, 0, 0, NH)
-        store(2, 0, 0, NH)
+        add_and_store(1, 0)
+        weigh_direct(2, 0)
+        quantize_modules(0, 1)
+        add_and_store(2, 0)
         product("direct", 4, 0, 7)
-        copy_d(2, 1, scopy)
-        weigh_direct(3, 0, 0, NH)
-        quantize_d(1, 1)
-        add_up(3, 0, 0, NH)
-        store(3, 0, 0, NH)
+        interleave(2, 1, on_scalar)
+        weigh_direct(3, 0)
+        quantize_modules(1, 1)
+        add_and_store(3, 0)
+
         product("walk", 0, 1, 0)
-        weigh_direct(4, 0, 0, NH)
-        copy_d(3, 1, vcopy, 0, 256)
-        add_up(4, 0, 0, NH)
-        store(4, 0, 0, NH)
+        weigh_direct(4, 0)
+        interleave(3, 1, on_vector, 0, SHARE)
+        add_and_store(4, 0)
         product("walk", 1, 1, 1)
-        restart(0, 1)
-        copy_d(3, 1, scopy, 256, 512)
-        quantize_d(2, 1)
+        keep_tanh(0, 1)
+        interleave(3, 1, on_scalar, SHARE, NH)
+        quantize_modules(2, 1)
         product("walk", 2, 1, 2)
-        restart(1, 1)
-        copy_d(4, 1, vcopy)
-        quantize_d(3, 1)
+        keep_tanh(1, 1)
+        interleave(4, 1, on_vector)
+        quantize_modules(3, 1)
         product("walk", 3, 1, 3)
-        restart(2, 1)
-        quantize_d(4, 1)
+        keep_tanh(2, 1)
+        quantize_modules(4, 1)
         weigh_far(0, 1)
         weigh_far(1, 1)
         product("walk", 4, 1, 4)
-        restart(3, 1)
+        keep_tanh(3, 1)
         weigh_far(2, 1)
+
         product("direct", 0, 1, 5)
-        restart(4, 1)
+        keep_tanh(4, 1)
         weigh_far(3, 1)
         for m in range(1, MT - 1):
-            product("direct", m, 1, (5 + m) % 8)
+            product("direct", m, 1, 5 + m)
             finish(m - 1, 1)
-        bank = 1
-        m, h = MT - 1, H - 1
-        r = r_sb[m, h]
-        nc.scalar.activation(out=r[:], in_=r[:], func=COPY, scale=-0.5, bias=0.5)
-        product("far", m, h, bank)
-        finish(m - 1, h)
-        tail = [(0, 256), (256, 384), (384, 512)]
-        for i, (c0, c1) in enumerate(tail):
-            product("direct", m, h, (bank + 1 + i) % 8, c0, c1)
-        nc.vector.scalar_tensor_tensor(
-            out=f_sb[m, h][:], in0=r[:], scalar=1.0, in1=acc["far", m, h, 0][:], op0=ALU.subtract, op1=ALU.mult
-        )
-        weighed = f_sb[0, 0]
 
-        def last_weigh(c0, c1):
+        m, h = MT - 1, H - 1
+        r = res_sb[m, h]
+        nc.scalar.activation(out=r[:], in_=r[:], func=COPY, scale=-0.5, bias=0.5)
+        product("far", m, h, 1)
+        finish(m - 1, h)
+        starts = range(0, NH, TAIL)
+        for bank, c in enumerate(starts, 2):
+            product("direct", m, h, bank, c, c + TAIL)
+        nc.vector.scalar_tensor_tensor(
+            out=far_sb[m, h][:], in0=r[:], scalar=1.0, in1=sums["far", m, h, 0][:], op0=ALU.subtract, op1=ALU.mult
+        )
+        weighed = far_sb[0, 0]
+
+        def weigh_last(c):
+            cols = slice(c, c + TAIL)
             nc.vector.tensor_tensor(
-                out=weighed[:, c0:c1], in0=acc["direct", m, h, c0][:, c0:c1], in1=r[:, c0:c1], op=ALU.mult
+                out=weighed[:, cols], in0=sums["direct", m, h, c][:, cols], in1=r[:, cols], op=ALU.mult
             )
 
-        def last_add(c0, c1):
-            nc.vector.tensor_tensor(out=r[:, c0:c1], in0=weighed[:, c0:c1], in1=f_sb[m, h][:, c0:c1], op=ALU.subtract)
+        def add_last(c):
+            cols = slice(c, c + TAIL)
+            nc.vector.tensor_tensor(out=r[:, cols], in0=weighed[:, cols], in1=far_sb[m, h][:, cols], op=ALU.subtract)
+            store(m, h, c, c + TAIL)
 
-        last_weigh(*tail[0])
-        last_weigh(*tail[1])
-        last_add(*tail[0])
-        store(m, h, *tail[0])
-        last_weigh(*tail[2])
-        last_add(*tail[1])
-        store(m, h, *tail[1])
-        last_add(*tail[2])
-        store(m, h, *tail[2])
+        weigh_last(0)
+        for c in starts[1:]:
+            weigh_last(c)
+            add_last(c - TAIL)
+        add_last(starts[-1])

@@ -164,6 +164,12 @@ def tile_drug_restart_scores_s10_kernel(
             for g in range(g0, g1):
                 sorted_chunks[m, g] = t[:, :, P * g : P * (g + 1)]
 
+        def sort_tile(m):
+            sort_pairs(m, 0, 1, on_vector)
+            sort_pairs(m, 1, 2, on_scalar)
+            sort_pairs(m, 2, LAST_G, on_vector)
+            sort_pairs(m, LAST_G, G, on_scalar)
+
         def transpose(piece, bank):
             turned[piece] = bank_tile([P, 2, 2, P], bank)
             for j, (m, g) in enumerate(piece):
@@ -328,9 +334,7 @@ def tile_drug_restart_scores_s10_kernel(
         transpose(mid0, 5)
         warm_up(2)
         group(head0, on_scalar)
-        sort_pairs(1, 0, 2, on_vector)
-        sort_pairs(1, LAST_G, G, on_scalar)
-        sort_pairs(1, 2, LAST_G, on_vector)
+        sort_tile(1)
         transpose(head1, 6)
         transpose(mid1, 7)
         transpose(ends, 4)
@@ -347,9 +351,7 @@ def tile_drug_restart_scores_s10_kernel(
         for m in range(2):
             for h in range(H):
                 open_sum("far", m, h, H * m + h)
-        sort_pairs(2, 0, 2, on_vector)
-        sort_pairs(2, LAST_G, G, on_scalar)
-        sort_pairs(2, 2, LAST_G, on_vector)
+        sort_tile(2)
         for m in range(2):
             for g in range(FAR_SPLIT):
                 far_passes(m, g)
@@ -381,7 +383,8 @@ def tile_drug_restart_scores_s10_kernel(
             transpose(piece, bank)
         product("far", 2, 1, 5)
         keep_far(1, 1)
-        for piece in (head3, mid3, head4, mid4):
+        group(head3, on_vector)
+        for piece in (mid3, head4, mid4):
             group(piece, on_scalar)
         quantize_seeds(head3)
         sort_quadrants()

@@ -327,7 +327,8 @@ def tile_drug_restart_scores_s10_kernel(
         head0, mid0 = pieces(0)[:2]
         head1, mid1 = pieces(1)[:2]
         ends = ((0, LAST_G), (1, LAST_G))
-        warm_up(2)
+        warm_up(3)
+        sort_pairs(0, 0, 2, on_vector)
         transpose(head0, 4)
         warm_up(2)
         sort_pairs(0, 2, G, on_vector)

@@ -327,7 +327,7 @@ def tile_drug_restart_scores_s10_kernel(
         head0, mid0 = pieces(0)[:2]
         head1, mid1 = pieces(1)[:2]
         ends = ((0, LAST_G), (1, LAST_G))
-        warm_up(3)
+        warm_up(2)
         sort_pairs(0, 0, 2, on_vector)
         transpose(head0, 4)
         warm_up(2)

@@ -333,7 +333,7 @@ def tile_drug_restart_scores_s10_kernel(
         warm_up(2)
         sort_pairs(0, 2, G, on_vector)
         transpose(mid0, 5)
-        warm_up(2)
+        warm_up(1)
         group(head0, on_scalar)
         sort_tile(1)
         transpose(head1, 6)

@@ -115,9 +115,6 @@ def tile_drug_restart_scores_s10_kernel(
 
         make_identity(nc, ident[:])
         nc.vector.memset(far_s[0][:].bitcast(I32), 0)
-        nc.vector.memset(far_s[1][:].bitcast(I32), 0)
-        nc.vector.memset(walk_s[0][:].bitcast(I32), 0)
-        nc.vector.memset(walk_s[1][:].bitcast(I32), 0)
         nc.vector.memset(mod_codes[:, LAST_G, 0:NH], 0)
         nc.vector.memset(mod_scales[:, LAST_G, 0:NH].bitcast(I32), 0)
 
@@ -327,13 +324,13 @@ def tile_drug_restart_scores_s10_kernel(
         head0, mid0 = pieces(0)[:2]
         head1, mid1 = pieces(1)[:2]
         ends = ((0, LAST_G), (1, LAST_G))
-        warm_up(2)
+        warm_up(3)
         sort_pairs(0, 0, 2, on_vector)
         transpose(head0, 4)
-        warm_up(2)
+        warm_up(1)
         sort_pairs(0, 2, G, on_vector)
         transpose(mid0, 5)
-        warm_up(1)
+        warm_up(2)
         group(head0, on_scalar)
         sort_tile(1)
         transpose(head1, 6)

@@ -327,7 +327,6 @@ def tile_drug_restart_scores_s10_kernel(
         warm_up(3)
         sort_pairs(0, 0, 2, on_vector)
         transpose(head0, 4)
-        warm_up(1)
         sort_pairs(0, 2, G, on_vector)
         transpose(mid0, 5)
         warm_up(2)

from contextlib import ExitStack

import concourse.mybir as mybir
from concourse.masks import make_identity

D, K, N = 640, 2560, 1024
FLOPS = 3 * 2 * D * K * N

F32 = mybir.dt.float32
BF16 = mybir.dt.bfloat16
U32 = mybir.dt.uint32
I32 = mybir.dt.int32
U8 = mybir.dt.uint8
E4M3 = mybir.dt.float8_e4m3fn_x4
E2M1 = mybir.dt.float4_e2m1fn_x4
ALU = mybir.AluOpType
TANH = mybir.ActivationFunctionType.Tanh
COPY = mybir.ActivationFunctionType.Copy

P = 128
QUAD = 32
GENES = 512
PAIRS = GENES // 2
G = K // GENES
LAST_G = G - 1
MT = D // P
NH = 512
H = N // NH
BANKS = 8
FAR_SPLIT = 3
SHARE = NH // 2
TAIL = 128


def tile_drug_restart_scores_s10_kernel(
    tc, seeds, far_words, far_scales, walk_words, walk_scales, modules, out
):
    nc = tc.nc
    with ExitStack() as ctx:
        keep = ctx.enter_context(tc.tile_pool(name="keep", bufs=1))
        stage = ctx.enter_context(tc.tile_pool(name="stage", bufs=2))
        psum = ctx.enter_context(tc.psum_pool(name="psum", bufs=1))
        ctx.enter_context(tc.manual_schedule())
        on_vector = nc.vector.tensor_copy
        on_scalar = nc.scalar.copy

        def kept(shape, dtype, name):
            return keep.tile(shape, dtype, name=name, align_bytes=256)

        def bank_tile(shape, bank):
            return psum.tile(shape, F32, name="bank%d" % bank)

        ident = kept([P, P], F32, "ident")
        far_w = [kept([P, 2 * N], U8, "far_w%d" % g) for g in range(G)]
        far_runs = [(0, FAR_SPLIT), (FAR_SPLIT, G)]
        far_s = [kept([P, g1 - g0, N], U8, "far_s%d" % g0) for g0, g1 in far_runs]
        walk_w = {}
        walk_s = [kept([P, N], U8, "walk_s%d" % i) for i in range(2)]
        mod_raw = [[kept([P, 4, NH], BF16, "mod_raw%d%d" % (g, h)) for h in range(H)] for g in range(G)]
        mod_codes = kept([P, G, N], U32, "mod_codes")
        mod_scales = kept([P, G, N], U8, "mod_scales")
        results = [(m, h) for h in range(H) for m in range(MT)]
        far_sb = {mh: kept([P, NH], F32, "far_sb%d%d" % mh) for mh in results}
        res_sb = {mh: kept([P, NH], F32, "res_sb%d%d" % mh) for mh in results}

        seeds_raw = {}

        def load_seeds(m, g0, g1):
            t = kept([P, GENES * (g1 - g0)], BF16, "seeds_raw%d%d" % (m, g0))
            nc.sync.dma_start(out=t[:], in_=seeds[m * P : (m + 1) * P, GENES * g0 : GENES * g1])
            for g in range(g0, g1):
                seeds_raw[m, g] = (t, g0)

        def load_seeds_by_quadrant():
            t = kept([P, 2 * P // QUAD, P], BF16, "seeds_raw00")
            rows = seeds[3 * P : 5 * P, GENES * LAST_G :].rearrange("(b i) (a c) -> i b a c", i=QUAD, c=P)
            for a in (0, 2, 1, 3):
                nc.sync.dma_start(out=t[QUAD * a : QUAD * (a + 1), :, :], in_=rows[:, :, a, :])
            return t

        def load_far(g):
            nc.sync.dma_start(out=far_w[g][:].bitcast(I32), in_=far_words.bitcast(I32)[g])

        def load_far_scales(run):
            g0, g1 = far_runs[run]
            for r in range(4):
                nc.sync.dma_start(
                    out=far_s[run][:].bitcast(I32)[r:P:QUAD, :, :],
                    in_=far_scales.bitcast(I32)[g0:g1, r:16:4, :].rearrange("g q w -> q g w"),
                )

        def load_walk(h):
            walk_w[h] = kept([P, G, NH], U32, "walk_w%d" % h)
            words = walk_words.rearrange("g p n t -> g p (n t)").bitcast(I32)
            nc.sync.dma_start(
                out=walk_w[h][:].bitcast(I32), in_=words[:, :, h * NH : (h + 1) * NH].rearrange("g p w -> p g w")
            )

        def load_walk_scales_packed():
            for q in range(4):
                nc.sync.dma_start(
                    out=walk_s[0][:].bitcast(I32)[QUAD * q : QUAD * q + 16, :],
                    in_=walk_scales.bitcast(I32)[0:LAST_G, 4 * q : 4 * q + 4, :],
                )

        def load_walk_scales_last():
            for r in range(4):
                nc.sync.dma_start(
                    out=walk_s[1][:].bitcast(I32)[r:P:QUAD, :], in_=walk_scales.bitcast(I32)[LAST_G, r:16:4, :]
                )

        def load_modules(g, h):
            rows = modules[GENES * g : GENES * (g + 1), h * NH : (h + 1) * NH]
            nc.sync.dma_start(out=mod_raw[g][h][:], in_=rows.rearrange("(p j) w -> p j w", j=4))

        make_identity(nc, ident[:])
        nc.vector.memset(far_s[0][:].bitcast(I32), 0)
        nc.vector.memset(mod_codes[:, LAST_G, 0:NH], 0)
        nc.vector.memset(mod_scales[:, LAST_G, 0:NH].bitcast(I32), 0)

        load_seeds(0, 0, 2)
        load_seeds(0, 2, G)
        load_seeds(1, 0, G)
        load_far_scales(0)
        for g in range(FAR_SPLIT):
            load_far(g)
        load_seeds(2, 0, G)
        load_far_scales(1)
        for g in range(FAR_SPLIT, G):
            load_far(g)
        load_seeds(3, 0, LAST_G)
        load_seeds(4, 0, LAST_G)
        quadrant_raw = load_seeds_by_quadrant()
        load_modules(0, 0)
        load_walk_scales_packed()
        load_walk(0)
        load_walk_scales_last()
        for g in range(1, G):
            load_modules(g, 0)
        for g in range(2):
            load_modules(g, 1)
        load_walk(1)
        for g in range(2, G):
            load_modules(g, 1)

        sorted_tiles = {}
        sorted_chunks = {}
        turned = {}
        grouped = {}
        stationary = {}

        def raw_pairs(m, g0, g1):
            t, base = seeds_raw[m, g0]
            return t[:].bitcast(F32)[:, PAIRS * (g0 - base) : PAIRS * (g1 - base)]

        def sort_pairs(m, g0, g1, copy):
            if m not in sorted_tiles:
                sorted_tiles[m] = stage.tile([P, 2, G * P], F32, name="seeds_sorted", align_bytes=256)
            t = sorted_tiles[m]
            copy(out=t[:, :, P * g0 : P * g1], in_=raw_pairs(m, g0, g1).rearrange("r (w u) -> r u w", u=2))
            for g in range(g0, g1):
                sorted_chunks[m, g] = t[:, :, P * g : P * (g + 1)]

        def sort_tile(m):
            sort_pairs(m, 0, 1, on_vector)
            sort_pairs(m, 1, 2, on_scalar)
            sort_pairs(m, 2, LAST_G, on_vector)
            sort_pairs(m, LAST_G, G, on_scalar)

        def transpose(piece, bank):
            turned[piece] = bank_tile([P, 2, 2, P], bank)
            for j, (m, g) in enumerate(piece):
                for u in range(2):
                    if (m, g) in sorted_chunks:
                        src = sorted_chunks[m, g][:, u, :]
                    else:
                        src = raw_pairs(m, g, g + 1)[:, u:PAIRS:2]
                    nc.tensor.transpose(turned[piece][:, j, u, :], src, ident[:])

        def grouped_tile(piece):
            grouped[piece] = stage.tile([P, 2, P, 4], BF16, name="seeds_grouped", align_bytes=256, bufs=4)
            return grouped[piece]

        def group(piece, copy):
            n = len(piece)
            t = grouped_tile(piece)
            copy(out=t[:].bitcast(F32)[:, 0:n], in_=turned[piece][:, 0:n, :, :].rearrange("p c u r -> p c r u"))

        def quantize_seeds(piece):
            n = len(piece)
            codes = kept([P, n * P], U32, "seeds_codes%d%d" % piece[0])
            scales = kept([P, n * P], U8, "seeds_scales%d%d" % piece[0])
            nc.vector.quantize_mx(
                out=codes[:].bitcast(E4M3),
                scales=scales[:],
                in_=grouped[piece][:, 0:n].rearrange("p c r j -> p (c r j)"),
            )
            for j, chunk in enumerate(piece):
                stationary[chunk] = (codes[:, j * P : (j + 1) * P], scales[:, j * P : (j + 1) * P])

        def pieces(m):
            return [((m, 0), (m, 1)), ((m, 2), (m, 3)), ((m, 4),)]

        quadrant_sorted = kept([P, 2, 2 * P], F32, "quadrant_sorted")
        quadrant_turned = kept([P, 2, 2 * P], F32, "quadrant_turned")

        def sort_quadrants():
            words = quadrant_raw[:].rearrange("p b c -> p (b c)").bitcast(F32)
            on_vector(out=quadrant_sorted[:], in_=words.rearrange("p (w u) -> p u w", u=2))

        def transpose_quadrants():
            nc.vector.transpose(
                quadrant_turned[:].rearrange("p u c -> p (u c)"), quadrant_sorted[:].rearrange("p u w -> p (u w)")
            )

        def group_quadrants(piece):
            words = grouped_tile(piece)[:].rearrange("p c r j -> p (c r j)").bitcast(F32)
            on_vector(out=words.rearrange("p (c u) -> p c u", u=2), in_=quadrant_turned[:].rearrange("p u c -> p c u"))

        mod_grouped = {}

        def interleave(g, h, copy, c0=0, c1=NH):
            if c0 == 0:
                mod_grouped[g, h] = stage.tile([P, NH, 4], BF16, name="mod_grouped", align_bytes=256, bufs=4)
            copy(
                out=mod_grouped[g, h][:, c0:c1, :].rearrange("p (c i) j -> p c j i", i=4),
                in_=mod_raw[g][h][:, :, c0:c1].rearrange("p j (c i) -> p c j i", i=4),
            )

        def quantize_modules(g, h):
            cols = slice(h * NH, (h + 1) * NH)
            nc.vector.quantize_mx(
                out=mod_codes[:, g, cols].bitcast(E4M3),
                scales=mod_scales[:, g, cols],
                in_=mod_grouped[g, h][:].rearrange("p w j -> p (w j)"),
            )

        sums = {}

        def open_sum(kind, m, h, bank, c0=0):
            sums[kind, m, h, c0] = bank_tile([P, NH], bank % BANKS)

        def one_pass(kind, m, h, g, c0=0, c1=NH):
            n0, n1 = h * NH + c0, h * NH + c1
            if kind == "far":
                rhs = far_w[g][:, 2 * n0 : 2 * n1].bitcast(E2M1)
                rhs_scale = far_s[g // FAR_SPLIT][:, g % FAR_SPLIT, n0:n1]
            elif kind == "walk":
                rhs = walk_w[h][:, g, c0:c1].bitcast(E4M3)
                rhs_scale = walk_s[g // LAST_G][4 * (g % LAST_G) :, n0:n1]
            else:
                rhs = mod_codes[:, g, n0:n1].bitcast(E4M3)
                rhs_scale = mod_scales[:, g, n0:n1]
            codes, scales = stationary[m, g]
            nc.tensor.matmul_mx(
                out=sums[kind, m, h, c0][:, c0:c1],
                lhsT=codes.bitcast(E4M3),
                lhsT_scale=scales,
                rhs=rhs,
                rhs_scale=rhs_scale,
                start=(g == 0),
                stop=(g == LAST_G),
            )

        def product(kind, m, h, bank, c0=0, c1=NH):
            open_sum(kind, m, h, bank, c0)
            for g in range(G):
                one_pass(kind, m, h, g, c0, c1)

        def far_passes(m, g):
            for h in range(H):
                one_pass("far", m, h, g)

        def warm_up(count):
            bank = bank_tile([P, NH], 3)
            for i in range(count):
                nc.tensor.matmul_mx(
                    out=bank[:],
                    lhsT=mod_codes[:, LAST_G, 0:P].bitcast(E4M3),
                    lhsT_scale=mod_scales[:, LAST_G, 0:P],
                    rhs=mod_codes[:, LAST_G, 0:NH].bitcast(E4M3),
                    rhs_scale=mod_scales[:, LAST_G, 0:NH],
                    start=True,
                    stop=True,
                )

        def keep_far(m, h):
            nc.scalar.activation(out=far_sb[m, h][:], in_=sums["far", m, h, 0][:], func=COPY, scale=0.5)

        def keep_tanh(m, h):
            nc.scalar.activation(out=res_sb[m, h][:], in_=sums["walk", m, h, 0][:], func=TANH, scale=0.5)

        def weigh_far(m, h):
            nc.vector.scalar_tensor_tensor(
                out=far_sb[m, h][:], in0=res_sb[m, h][:], scalar=1.0, in1=far_sb[m, h][:], op0=ALU.add, op1=ALU.mult
            )

        def weigh_direct(m, h, c0=0, c1=NH):
            r = res_sb[m, h][:, c0:c1]
            nc.vector.scalar_tensor_tensor(
                out=r, in0=r, scalar=1.0, in1=sums["direct", m, h, 0][:, c0:c1], op0=ALU.subtract, op1=ALU.mult
            )

        def add_up(m, h, c0=0, c1=NH):
            r = res_sb[m, h][:, c0:c1]
            nc.vector.scalar_tensor_tensor(
                out=r, in0=r, scalar=-0.5, in1=far_sb[m, h][:, c0:c1], op0=ALU.mult, op1=ALU.add
            )

        def store(m, h, c0=0, c1=NH):
            nc.sync.dma_start(out=out[m * P : (m + 1) * P, h * NH + c0 : h * NH + c1], in_=res_sb[m, h][:, c0:c1])

        def add_and_store(m, h):
            add_up(m, h)
            store(m, h)

        def finish(m, h):
            for c0 in (0, NH // 2):
                weigh_direct(m, h, c0, c0 + NH // 2)
            for c0 in (0, NH // 2):
                add_up(m, h, c0, c0 + NH // 2)
            store(m, h)

        head0, mid0 = pieces(0)[:2]
        head1, mid1 = pieces(1)[:2]
        ends = ((0, LAST_G), (1, LAST_G))
        warm_up(3)
        sort_pairs(0, 0, 2, on_vector)
        transpose(head0, 4)
        sort_pairs(0, 2, G, on_vector)
        transpose(mid0, 5)
        warm_up(2)
        group(head0, on_scalar)
        sort_tile(1)
        transpose(head1, 6)
        transpose(mid1, 7)
        transpose(ends, 4)
        group(mid0, on_scalar)
        quantize_seeds(head0)
        group(head1, on_vector)
        group(mid1, on_scalar)
        quantize_seeds(mid0)
        quantize_seeds(head1)
        group(ends, on_scalar)
        quantize_seeds(mid1)
        quantize_seeds(ends)

        for m in range(2):
            for h in range(H):
                open_sum("far", m, h, H * m + h)
        sort_tile(2)
        for m in range(2):
            for g in range(FAR_SPLIT):
                far_passes(m, g)
        head2, mid2, end2 = pieces(2)
        for bank, piece in enumerate((head2, mid2, end2), 5):
            transpose(piece, bank)
        group(head2, on_vector)
        group(mid2, on_scalar)
        quantize_seeds(head2)
        group(end2, on_vector)
        quantize_seeds(mid2)
        quantize_seeds(end2)
        sort_pairs(3, 0, 2, on_scalar)
        sort_pairs(3, 2, LAST_G, on_vector)
        for g in range(FAR_SPLIT, G):
            for m in range(2):
                far_passes(m, g)
        sort_pairs(4, 0, 2, on_vector)
        sort_pairs(4, 2, LAST_G, on_vector)
        keep_far(0, 0)
        keep_far(0, 1)
        keep_far(1, 0)

        head3, mid3 = pieces(3)[:2]
        head4, mid4 = pieces(4)[:2]
        by_quadrant = ((3, LAST_G), (4, LAST_G))
        product("far", 2, 0, 4)
        for piece, bank in zip((head3, mid3, head4, mid4), (6, 7, 0, 1)):
            transpose(piece, bank)
        product("far", 2, 1, 5)
        keep_far(1, 1)
        group(head3, on_vector)
        for piece in (mid3, head4, mid4):
            group(piece, on_scalar)
        quantize_seeds(head3)
        sort_quadrants()
        quantize_seeds(mid3)
        transpose_quadrants()
        quantize_seeds(head4)
        group_quadrants(by_quadrant)
        quantize_seeds(mid4)
        quantize_seeds(by_quadrant)
        keep_far(2, 0)
        keep_far(2, 1)
        late = ((3, 0, 3), (3, 1, 2), (4, 0, 4))
        for m, h, bank in late:
            open_sum("far", m, h, bank)
            for g in range(LAST_G):
                one_pass("far", m, h, g)
        for m, h, bank in late:
            one_pass("far", m, h, LAST_G)

        interleave(0, 0, on_vector)
        product("walk", 0, 0, 6)
        for m, h, bank in late:
            keep_far(m, h)
        quantize_modules(0, 0)
        interleave(1, 0, on_vector)
        product("walk", 1, 0, 7)
        keep_tanh(0, 0)
        interleave(2, 0, on_scalar, 0, SHARE)
        quantize_modules(1, 0)
        interleave(2, 0, on_vector, SHARE, NH)
        product("walk", 2, 0, 0)
        keep_tanh(1, 0)
        interleave(3, 0, on_scalar, 0, SHARE)
        weigh_far(0, 0)
        interleave(3, 0, on_vector, SHARE, NH)
        quantize_modules(2, 0)
        product("walk", 3, 0, 1)
        interleave(4, 0, on_scalar, 0, SHARE)
        interleave(4, 0, on_vector, SHARE, NH)
        quantize_modules(3, 0)
        weigh_far(1, 0)
        quantize_modules(4, 0)
        keep_tanh(2, 0)
        product("walk", 4, 0, 2)
        keep_tanh(3, 0)
        keep_tanh(4, 0)

        interleave(0, 1, on_scalar, 0, SHARE)
        for m in range(2):
            open_sum("direct", m, 0, 3 + m)
        for g in range(G):
            for m in range(2):
                one_pass("direct", m, 0, g)
        for m in range(2, MT):
            weigh_far(m, 0)
        interleave(0, 1, on_scalar, SHARE, NH)
        interleave(1, 1, on_scalar)
        product("direct", 2, 0, 5)
        weigh_direct(0, 0)
        weigh_direct(1, 0)
        add_and_store(0, 0)
        product("direct", 3, 0, 6)
        add_and_store(1, 0)
        weigh_direct(2, 0)
        quantize_modules(0, 1)
        add_and_store(2, 0)
        product("direct", 4, 0, 7)
        interleave(2, 1, on_scalar)
        weigh_direct(3, 0)
        quantize_modules(1, 1)
        add_and_store(3, 0)

        product("walk", 0, 1, 0)
        weigh_direct(4, 0)
        interleave(3, 1, on_vector, 0, SHARE)
        add_and_store(4, 0)
        product("walk", 1, 1, 1)
        keep_tanh(0, 1)
        interleave(3, 1, on_scalar, SHARE, NH)
        quantize_modules(2, 1)
        product("walk", 2, 1, 2)
        keep_tanh(1, 1)
        interleave(4, 1, on_vector)
        quantize_modules(3, 1)
        product("walk", 3, 1, 3)
        keep_tanh(2, 1)
        quantize_modules(4, 1)
        weigh_far(0, 1)
        weigh_far(1, 1)
        product("walk", 4, 1, 4)
        keep_tanh(3, 1)
        weigh_far(2, 1)

        product("direct", 0, 1, 5)
        keep_tanh(4, 1)
        weigh_far(3, 1)
        for m in range(1, MT - 1):
            product("direct", m, 1, 5 + m)
            finish(m - 1, 1)

        m, h = MT - 1, H - 1
        r = res_sb[m, h]
        nc.scalar.activation(out=r[:], in_=r[:], func=COPY, scale=-0.5, bias=0.5)
        product("far", m, h, 1)
        finish(m - 1, h)
        starts = range(0, NH, TAIL)
        for bank, c in enumerate(starts, 2):
            product("direct", m, h, bank, c, c + TAIL)
        nc.vector.scalar_tensor_tensor(
            out=far_sb[m, h][:], in0=r[:], scalar=1.0, in1=sums["far", m, h, 0][:], op0=ALU.subtract, op1=ALU.mult
        )
        weighed = far_sb[0, 0]

        def weigh_last(c):
            cols = slice(c, c + TAIL)
            nc.vector.tensor_tensor(
                out=weighed[:, cols], in0=sums["direct", m, h, c][:, cols], in1=r[:, cols], op=ALU.mult
            )

        def add_last(c):
            cols = slice(c, c + TAIL)
            nc.vector.tensor_tensor(out=r[:, cols], in0=weighed[:, cols], in1=far_sb[m, h][:, cols], op=ALU.subtract)
            store(m, h, c, c + TAIL)

        weigh_last(0)
        for c in starts[1:]:
            weigh_last(c)
            add_last(c - TAIL)
        add_last(starts[-1])
